import numpy as np, ml_dtypes
CORES = [3,11,19,27,35,43,51,59]
N = 8
import mx_ref
BF = ml_dtypes.bfloat16
def gentries(a):
    return np.ascontiguousarray(a.reshape(8, 16, -1).transpose(0, 2, 1)).reshape(8, -1)
def gtable(e):
    e = np.asarray(e); return np.ascontiguousarray(e.reshape(8, -1, 16).transpose(0, 2, 1)).reshape(128, -1).astype(np.int32)
def gcols(t, e):
    v = np.concatenate([t.reshape(8, 16, -1, 4), np.zeros((8, 16, 1, 4), BF)], axis=2)
    return np.ascontiguousarray(np.stack([v[g][:, e[g]] for g in range(8)])).reshape(128, -1)
def tile(rs):
    return np.stack(rs, axis=2).reshape(128, -1).astype(BF)
def cut(t, i, w=512):
    return t[:, w * i:w * i + w]
def pick(q, e):
    c = np.concatenate([q[0].reshape(128, -1, 4), np.zeros((128, 1, 4), np.uint8)], axis=1); s = np.concatenate([q[1], np.ones((16, 1), np.uint8)], axis=1)
    return (np.ascontiguousarray(c[:, e].reshape(128, -1)), np.ascontiguousarray(s[:, e]))
def join(*qs):
    return (np.concatenate([q[0] for q in qs], axis=1), np.concatenate([q[1] for q in qs], axis=1))
def put(q, e, v):
    c, s = q[0].reshape(128, -1, 4).copy(), q[1].copy(); c[:, e] = v[0].reshape(128, -1, 4); s[:, e] = v[1]
    return (c.reshape(128, -1), s)
def pk(c, s):
    return (np.ascontiguousarray(c), mx_ref.live(s))
def emit(q):
    return q[0], q[1]
def packed(v, rng):
    q = [mx_ref.quantize(np.ascontiguousarray(v[r])) for r in range(N)]
    return np.stack([a for a, b in q]), np.stack([mx_ref.plane(b, rng) for a, b in q])
def values_of_codes():
    e, c = np.zeros((128, 128, 4), np.float32), np.zeros((128, 2, 4), np.uint8)
    e[np.arange(128), np.arange(128), 0] = 1
    c[:127, :, 0] = np.arange(256).reshape(2, 128).T[:127]
    return mx_ref.matmul(mx_ref.quantize(e.reshape(128, 512).astype(BF)), (c.reshape(128, 8), np.full((16, 2), 127, np.uint8))).T.reshape(-1).astype(np.float64)
CODE_VALUE, SCALE_VALUE = values_of_codes(), 2.0 ** (np.arange(256) - 127.0)
def decode(q):
    return (CODE_VALUE[q[0]].reshape(16, 8, -1, 4) * SCALE_VALUE[q[1]][:, None, :, None] + 0.0).reshape(128, -1).astype(np.float32)
def f(rng, *shape):
    return mx_ref.flush((rng.standard_normal(shape, dtype=np.float32) * np.exp2(rng.integers(-2, 3, shape[:-1] + (1,)))).astype(BF))
def wide(rng, *shape, cols=0):
    v = rng.standard_normal(shape, dtype=np.float32) * np.exp2(rng.integers(-12, 13, shape)).astype(np.float32)
    if cols: v *= np.repeat(np.exp2(rng.integers(-cols, cols + 1, shape[:-2] + (1, shape[-1] // 4))) * (rng.random(shape[:-2] + (1, shape[-1] // 4)) > 0.0625), 4, axis=-1).astype(np.float32)
    return mx_ref.flush(v.astype(BF))
C, L, R = 512, 384, 3
def read(pool, at, up):
    a = gcols(pool, at).astype(np.float32)
    b = gcols(pool, np.take_along_axis(up, at, axis=1)).astype(np.float32)
    return mx_ref.quantize(np.ascontiguousarray((a + b).astype(BF)))
def big(v):
    v = v.astype(np.float32)
    v[np.abs(v) < np.float32(2.0 ** -16)] = 0
    return v.astype(BF)
def numbers_of(rng):
    return {"x": big(f(rng, N, 128, 4 * C)), "u": np.array(f(rng, N, 128, 512))}
def listed(p, t):
    return {"par": np.stack([gtable(a) for a in p]), "top": np.stack([gtable(a) for a in t])}
def parents(rng):
    return np.where(rng.random((N, 8, C)) < 0.125, np.arange(C), rng.integers(0, C, (N, 8, C)))
def tops(rng):
    return rng.integers(0, C, (N, 8, L))
def among(rng, k, h):
    o = np.argsort(k, kind="stable")
    return o[rng.integers(np.searchsorted(k[o], h), np.searchsorted(k[o], h, side="right"))]
def weights(rng, w):
    c, p = packed(w, rng)
    return {"wc": c, "ws": p}
def still(rng, k):
    w = np.zeros((N, 128, 4, 128, 4), np.float32)
    i = np.arange(128)
    for b in range(4): w[:, i, b, i, b] = k
    return weights(rng, w.reshape(N, 128, 2048).astype(BF))
def signs(rng):
    return np.stack([rng.permutation(8) % 2 * 2.0 - 1.0 for r in range(N)])
def setup_inputs(rng):
    return {**numbers_of(rng), **listed(parents(rng), tops(rng)), **weights(rng, f(rng, N, 128, 2048))}
def setup_inputs_ties(rng):
    d = numbers_of(rng)
    e = rng.permutation(N)
    x = d["x"].reshape(N, 8, 16, C, 4)
    p, q = parents(rng), tops(rng)
    for r in range(N):
        k, h = (np.zeros(C, int), np.zeros(L, int)) if r == e[0] else (rng.permutation(C) % 3, rng.permutation(L) % 3)
        a = x[r][:, :8, :3].copy()
        a[:, :, 2] = 0
        x[r][:, :8] = a[:, :, k]
        p[r] = among(rng, k, np.tile(k, (8, 1)))
        q[r] = among(rng, k, np.tile(h, (8, 1)))
    x[e[1]] = 0
    u = d["u"].reshape(N, 8, 16, 128, 4)
    u[:, :, 8:, ::16] = 0
    w = np.array(f(rng, N, 128, 2048)).reshape(N, 8, 16, 4, 8, 16, 4)
    w[:, :, :, :, :, :8] = 0
    return {"x": x.reshape(N, 128, 4 * C), "u": u.reshape(N, 128, 512), **listed(p, q), **weights(rng, w.reshape(N, 128, 2048))}
def setup_inputs_near(rng):
    d = numbers_of(rng)
    x = d["x"].astype(np.float32).reshape(N, 8, 16, C, 4)
    m = np.arange(C) // 2
    g = ((m[:, None] >> np.arange(8)) & 1) * np.exp2(np.arange(8) - 23.0)
    a = np.repeat(rng.choice([-0.5, 0.5], (N, 8, C // 2)), 2, axis=-1)
    s = np.repeat(rng.choice([-1.0, 1.0], (N, 8, C // 2)), 2, axis=-1)
    x[:, :, 0] = 0
    x[:, :, 0, :, 0] = a
    x[:, :, 8] = g[:, :4] * s[..., None]
    x[:, :, 9] = g[:, 4:] * s[..., None]
    x[:, :, 10:] = rng.integers(4, 8, (N, 8, 6, C, 4)) * rng.choice([-1.0, 1.0], (N, 8, 6, C, 4)) * 2.0 ** -20
    u = d["u"].reshape(N, 128, 128, 4)
    one = rng.permutation(N) % 2 == 0
    x *= np.where(one, 1.0, 2.0 ** -6).astype(np.float32)[:, None, None, None, None]
    k = np.where(one, 1.0, 2.0 ** -30).astype(np.float32).astype(BF)
    u[:, :, ::16] = 0
    for h in range(0, 128, 16):
        u[:, h, h, 0] = k
        u[:, h + 8:h + 10, h] = k[:, None, None]
    p = np.repeat(rng.integers(0, C, (N, 8, C // 2)), 2, axis=-1)
    q = rng.permuted(np.tile(np.arange(C), (N, 8, 1)), axis=-1)[:, :, :L]
    return {"x": x.reshape(N, 128, 4 * C).astype(BF), "u": u.reshape(N, 128, 512), **listed(p, q), **still(rng, 64)}
def setup_inputs_huge(rng):
    d = numbers_of(rng)
    x = 2.0 ** 28 * (1.25 + 0.5 * rng.random((N, 128, C, 4)))
    one = rng.permutation(N) < N // 2
    p, q = parents(rng), tops(rng)
    for r in range(N):
        k, h = (np.zeros(C, int), np.zeros(L, int)) if one[r] else (rng.permutation(C) % 2, rng.permutation(L) % 2)
        x[r] *= (1.0 - 2.0 * k)[None, :, None]
        p[r] = among(rng, k, np.tile(k, (8, 1)))
        q[r] = among(rng, k, np.tile(h, (8, 1)))
    u = d["u"].reshape(N, 128, 128, 4)
    a = 2.0 ** 30 * (1 - 0.25 * rng.random((N, 128, 8, 4))) * signs(rng)[:, None, :, None]
    u[:, :, ::16] = a.astype(np.float32).astype(BF)
    return {"x": x.astype(np.float32).reshape(N, 128, 4 * C).astype(BF), "u": u.reshape(N, 128, 512), **listed(p, q), **still(rng, 16)}
def setup_inputs_forest(rng):
    d = setup_inputs(rng)
    p, q = parents(rng), tops(rng)
    e = rng.permutation(N)
    p[e[0]] = np.arange(C)
    p[e[1]] = rng.integers(0, C, (8, 1))
    p[e[2]] = (np.arange(C) + 1) % C
    q[e[3]] = rng.integers(0, C, (8, 1))
    return {**d, **listed(p, q)}
def setup_inputs_spread(rng):
    d = setup_inputs(rng)
    d["x"] = big(wide(rng, N, 128, 4 * C, cols=6))
    return d
def check_inputs(d):
    b = []
    for k in ("x", "u"):
        a = np.abs(d[k].astype(np.float32))
        if not (np.isfinite(a).all() and ((a == 0) | (a >= 2.0 ** -30) & (a <= 2.0 ** 30)).all()): b.append("a value of " + k)
    for k in ("par", "top"):
        if not ((d[k] >= 0) & (d[k] < C)).all(): b.append("an entry of " + k)
    return b
def reference(x, u, par, top, wc, ws):
    qu = [mx_ref.quantize(u[r]) for r in range(N)]
    lay = [pk(wc[r], ws[r]) for r in range(N)]
    pool = [x[r] for r in range(N)]
    up = [gentries(par[r]) for r in range(N)]
    at = [gentries(top[r]) for r in range(N)]
    for t in range(R):
        score, sent = [], []
        for r in range(N):
            q = read(pool[r], at[r], up[r])
            score.append(mx_ref.matmul(qu[r], q)[::16] + np.float32(0.0))
            sent.append(mx_ref.quantize(tile([np.maximum(mx_ref.matmul(pick(lay[r], np.arange(128 * b, 128 * b + 128)), q), np.float32(0.0)) * np.float32(0.015625) for b in range(4)])))
        came = decode(join(*sent)).astype(BF)
        for r in range(N):
            n = np.where(score[r] >= 0, C + L * t + np.arange(L), np.take_along_axis(up[r], at[r], axis=1))
            o = np.argsort(-score[r], axis=1, kind="stable")
            pool[r] = np.concatenate([pool[r], cut(came, (r - 1) % N, 4 * L)], axis=1)
            up[r] = np.concatenate([up[r], at[r]], axis=1)
            at[r] = np.take_along_axis(n, o, axis=1)
    y, ol = np.zeros((N, 128, L), np.float32), np.zeros((N, 8, L), np.float32)
    oc, osc = np.zeros((N, 128, 4 * L), np.uint8), np.zeros((N, 16, L), np.uint8)
    for r in range(N):
        q = read(pool[r], at[r], up[r])
        y[r] = mx_ref.matmul(qu[r], q)
        ol[r] = at[r]
        oc[r], osc[r] = emit(q)
    return {"y": y, "ol": ol, "oc": oc, "osc": osc}

@@ -1,0 +1,359 @@
+from concourse.mybir import dt, AluOpType, ActivationFunctionType
+
+A = AluOpType
+F = ActivationFunctionType
+C, L, R = 512, 384, 3
+J = L // 16
+NODES = C + R * L
+JV = (15, 15, 15)
+AHEAD = ((1, 2), (0, 1), ())
+DB = ("pb2", "pb3", "pb4", "pb6")
+JMAX = max(JV)
+SMAX = J - min(JV)
+UP = NODES
+ROW = [UP + C + L * t for t in range(R + 1)]
+STEP = 4096.0
+
+SCRATCH = {
+    "xs": ("sbuf", [128, 4 * C], "bfloat16"), "us": ("sbuf", [128, 512], "bfloat16"),
+    "pars": ("sbuf", [128, 32], "int32"), "tops": ("sbuf", [128, J], "int32"),
+    "wq": ("sbuf", [128, 512], "float8_e4m3fn_x4"), "wp": ("sbuf", [128, 512], "uint8"),
+    "uq": ("sbuf", [128, 128], "float8_e4m3fn_x4"), "up": ("sbuf", [128, 128], "uint8"),
+    "vq": ("sbuf", [128, 128], "float8_e4m3fn_x4"), "vp": ("sbuf", [128, 128], "uint8"),
+    "et": ("sbuf", [128, 520], "bfloat16"),
+    "eq": ("sbuf", [128, 512], "float8_e4m3fn_x4"), "ep": ("sbuf", [128, 512], "uint8"),
+    "z": ("sbuf", [128, 4 * L], "bfloat16"), "h": ("sbuf", [128, 4 * L], "bfloat16"),
+    "a0": ("sbuf", [128, 4 * L], "bfloat16"),
+    "tb": ("sbuf", [128, ROW[R] + L], "float32"),
+    "itp": ("sbuf", [128, L], "int32"), "res": ("sbuf", [128, L], "int32"), "i16": ("sbuf", [128, J], "int32"),
+    "mask": ("sbuf", [128, L], "bfloat16"), "keep": ("sbuf", [128, L], "bfloat16"), "kmin": ("sbuf", [128, L], "bfloat16"),
+    "keep3": ("sbuf", [128, 3 * SMAX], "float32"), "cols": ("sbuf", [128, 8], "float32"),
+    "lane": ("sbuf", [128, J], "float32"),
+    "uoff": ("sbuf", [128, 8], "uint16"), "po1": ("sbuf", [128, 32], "uint16"),
+    "noff": ("sbuf", [128, J], "uint16"), "roff": ("sbuf", [128, J], "uint16"),
+    "tpf": ("sbuf", [128, J], "float32"), "la": ("sbuf", [128, J], "float32"), "lb": ("sbuf", [128, J], "float32"),
+    "lc": ("sbuf", [128, J], "float32"), "cc": ("sbuf", [128, J], "float32"),
+    "mk": ("sbuf", [128, L], "float32"), "hold": ("sbuf", [128, L], "float32"),
+    "same": ("sbuf", [128, L], "bfloat16"), "cq": ("sbuf", [128, L], "bfloat16"),
+    "cmp": ("sbuf", [128, L * JMAX], "bfloat16"), "cnt": ("sbuf", [128, (L // 2) * JMAX], "bfloat16"),
+    "sgn": ("sbuf", [128, L * SMAX], "bfloat16"),
+    "ab": ("sbuf", [128, 3 * SMAX], "float32"), "ab2": ("sbuf", [128, 3 * SMAX], "float32"),
+    "nrow": ("sbuf", [128, L], "float32"), "held": ("sbuf", [128, L], "float32"),
+    "ya": ("sbuf", [128, L // 2], "float32"), "yb": ("sbuf", [128, L // 2], "float32"),
+}
+for _b in range(4):
+    SCRATCH["sp%d" % _b] = ("sbuf", [128, NODES], "bfloat16")
+    SCRATCH["pp%d" % _b] = ("sbuf", [128, C + 2 * L], "bfloat16")
+for _t in range(R + 1):
+    SCRATCH["zq%d" % _t] = ("sbuf", [128, L], "float8_e4m3fn_x4")
+    SCRATCH["zp%d" % _t] = ("sbuf", [128, L], "uint8")
+    SCRATCH["toff%d" % _t] = ("sbuf", [128, J], "uint16")
+for _t in range(R):
+    for _n in ("hq", "lq"):
+        SCRATCH["%s%d" % (_n, _t)] = ("sbuf", [128, L], "float8_e4m3fn_x4")
+    for _n in ("hp", "lp"):
+        SCRATCH["%s%d" % (_n, _t)] = ("sbuf", [128, L], "uint8")
+for _b in range(7):
+    SCRATCH["pb%d" % _b] = ("psum", [128, 512], "float32")
+
+NDMA = 16
+SEMAPHORES = ["sV", "sS", "sP", "sG", "sent"] + ["arr%d" % _t for _t in range(R)] + ["d%d" % _k for _k in range(NDMA)]
+
+
+def orderer(g, T):
+    queue = {"V": g.vector, "S": g.scalar, "P": g.tensor, "G": g, "Y": g.sync}
+    known = {q: {} for q in queue}
+    count, clock, writer, readers = {}, {}, {}, {}
+    ndma = [0]
+
+    def wait(q, marks):
+        need = {}
+        for sem, c in marks:
+            need[sem] = max(need.get(sem, 0), c)
+        for sem, c in sorted(need.items(), key=lambda e: -len(clock[e])):
+            if known[q].get(sem, 0) >= c:
+                continue
+            queue[q].wait_ge(T.sem[sem], c)
+            for s2, c2 in clock[(sem, c)].items():
+                known[q][s2] = max(known[q].get(s2, 0), c2)
+
+    def before(q, reads, writes):
+        marks = []
+        for k in reads:
+            if k in writer:
+                marks.append(writer[k])
+            if k.startswith("pb"):
+                marks += [m for m in readers.get(k, []) if m[0] != "s" + q]
+        for k in writes:
+            if k in writer and not (q == "P" and writer[k][0] == "sP"):
+                marks.append(writer[k])
+            marks += readers.get(k, [])
+        wait(q, marks)
+
+    def after(q, sem, n, reads, writes):
+        count[sem] = count.get(sem, 0) + n
+        mark = (sem, count[sem])
+        clock[mark] = dict(known[q])
+        clock[mark][sem] = count[sem]
+        for k in reads:
+            readers.setdefault(k, []).append(mark)
+        for k in writes:
+            writer[k] = mark
+            readers[k] = []
+
+    def op(q, call, reads, writes):
+        before(q, reads, writes)
+        call(queue[q]).then_inc(T.sem["s" + q], 1)
+        after(q, "s" + q, 1, reads, writes)
+
+    def dma(q, out, in_, reads, writes):
+        sem = "d%d" % ndma[0]
+        ndma[0] += 1
+        before(q, reads, writes)
+        queue[q].dma_start(out, in_).then_inc(T.sem[sem], 16)
+        after(q, sem, 16, reads, writes)
+
+    def remote(call, n, reads):
+        before("G", reads, [])
+        call()
+        after("G", "sent", n, [], [])
+
+    def arrival(sem, n, key):
+        count[sem] = n
+        clock[(sem, n)] = {sem: n}
+        writer[key] = (sem, n)
+
+    def finish(q):
+        wait(q, list(count.items()))
+
+    return op, dma, remote, arrival, finish
+
+
+def rank_program(g, core, T, topo):
+    rank = T.rank_of(core)
+    if rank is None:
+        return
+    n = len(T.cores)
+    nxt, prv = T.cores[(rank + 1) % n], T.cores[(rank - 1) % n]
+    rid, pid, _ = topo.addr(nxt)
+    engines = topo.mask(core, nxt)
+    n_out, n_in = len(topo.engines(core, nxt)), len(topo.engines(prv, core))
+    op, dma, remote, arrival, finish = orderer(g, T)
+    u8, u32 = dt.uint8, dt.uint32
+    last = slice(15, L, 16)
+    hl = L // 2
+
+    def ts(out, in0, s1, o0, s2=None, o1=None, r=(), w=()):
+        if o1 is None:
+            op("V", lambda e: e.tensor_scalar(out, in0, s1, None, o0), r, w)
+        else:
+            op("V", lambda e: e.tensor_scalar(out, in0, s1, s2, o0, o1), r, w)
+
+    def tt(out, in0, in1, o, r, w):
+        op("V", lambda e: e.tensor_tensor(out, in0, in1, o), r, w)
+
+    def scan(out, d0, d1, init, o0, o1, r, w):
+        op("V", lambda e: e.tensor_tensor_scan(out, d0, d1, init, o0, o1), r, w)
+
+    def copy(q, out, in_, r, w):
+        if q == "V":
+            op("V", lambda e: e.tensor_copy(out, in_), r, w)
+        else:
+            op("S", lambda e: e.activation(out, in_, F.Copy), r, w)
+
+    def quant(out, scales, in_, r, w):
+        op("V", lambda e: e.quantize_mx(out, scales, in_), r, w)
+
+    def mm(bank, cols, lq, lp, rq, rp, r):
+        op("P", lambda e: e.matmul_mx(T[bank][:, 0:cols], lq, lp, rq, rp, True, True), r, [bank])
+
+    def count_up(out, cols, base, w):
+        op("G", lambda e: e.iota(out, [[1, cols]], base, 0, allow_small_or_imprecise_dtypes=True), [], w)
+
+    dma("S", T.pars[:], T.par[:], [], ["pars"])
+    dma("Y", T.xs[:], T.x[:], [], ["xs"])
+    dma("Y", T.tops[:], T.top[:], [], ["tops"])
+    dma("Y", T.us[:], T.u[:], [], ["us"])
+    dma("Y", T.wq[:].bitcast(u8), T.wc[:], [], ["wq"])
+    dma("Y", T.wp[:], T.ws[:], [], ["wp"])
+
+    op("G", lambda e: e.iota(T.itp[:], [[1, L]], 128, -1), [], ["itp"])
+    op("G", lambda e: e.iota(T.i16[:], [[16, J]], 0, 0), [], ["i16"])
+    count_up(T.tb[:, 0:C], C, 0, ["tb0"])
+    op("V", lambda e: e.memset(T.et[:], 0.0), [], ["et"])
+    op("V", lambda e: e.memset(T.keep3[:], 1.0), [], ["keep3"])
+    op("V", lambda e: e.memset(T.ab[:], 0.0), [], ["ab"])
+    ts(T.keep3[:, 0:3 * SMAX:3], T.keep3[:, 0:3 * SMAX:3], 0.0, A.mult, r=["keep3"], w=["keep3"])
+    ts(T.res[:], T.itp[:], 15, A.bitwise_and, r=["itp"], w=["res"])
+    ts(T.et[:, 3:515:4], T.itp[:, 0:128], 128.0, A.is_equal, r=["itp", "et"], w=["et"])
+    ts(T.mask[:], T.res[:], 0.0, A.is_equal, r=["res"], w=["mask"])
+    ts(T.cols[:, 0:1], T.res[:, 15:16], STEP, A.mult, r=["res"], w=["colv"])
+    ts(T.cols[:, 1:2], T.res[:, 15:16], -1.0, A.mult, 15.0, A.add, r=["res"], w=["colp"])
+    copy("V", T.uoff[:], T.i16[:, 0:8], ["i16"], ["uoff"])
+    op("S", lambda e: e.activation(T.keep[:], T.mask[:], F.Identity, bias=1.0, scale=-1.0), ["mask"], ["keep"])
+    op("S", lambda e: e.activation(T.kmin[:], T.mask[:], F.Identity, bias=-STEP, scale=18 * STEP), ["mask"], ["kmin"])
+    ts(T.lane[:], T.i16[:], T.cols[:, 1:2], A.add, r=["i16", "colp"], w=["lane"])
+    copy("V", T.po1[:], T.pars[:], ["pars"], ["po1"])
+    for b in range(4):
+        quant(T.eq[:, 128 * b:128 * b + 128], T.ep[:, 128 * b:128 * b + 128], T.et[:, 3 - b:515 - b], ["et"], ["eq%d" % b])
+    copy("S", T.tb[:, UP:UP + C], T.tb[:, 0:C].indirect(T.po1[:]), ["tb0", "po1"], ["par"])
+
+    def gather_z(q, t, b):
+        copy(q, T.z[:, b:4 * L:4], T["sp%d" % b][:, 0:C + L * t].indirect(T["toff%d" % t][:]),
+             ["sp%d" % b, "toff%d" % t], ["z%d" % b])
+
+    def gather_top(t, b):
+        copy("S", T.a0[:, L * b:L * b + L], T["pp%d" % b][:, 0:C + L * t].indirect(T["toff%d" % t][:]),
+             ["pp%d" % b, "toff%d" % t], ["a0%d" % b])
+
+    copy("V", T.pp0[:, 0:C], T.xs[:, 0:4 * C:4], ["xs"], ["pp0"])
+    copy("V", T.toff0[:], T.tops[:], ["tops"], ["toff0"])
+    copy("S", T.pp1[:, 0:C], T.xs[:, 1:4 * C:4], ["xs"], ["pp1"])
+    for b in (2, 3):
+        op("G", lambda e, b=b: e.affine_select(T["pp%d" % b][:, 0:C], T.xs[:, b:4 * C:4], [[1, C]], A.is_ge, 0.0, 0, 0),
+           ["xs"], ["pp%d" % b])
+    count_up(T.tb[:, C:UP], UP - C, C, ["tb1"])
+    for b in range(4):
+        tt(T["sp%d" % b][:, 0:C], T["pp%d" % b][:, 0:C].indirect(T.po1[:]), T.xs[:, b:4 * C:4], A.add,
+           ["xs", "po1", "pp%d" % b], ["sp%d" % b])
+        if b == 0:
+            gather_top(0, b)
+        gather_z("S", 0, b)
+    quant(T.uq[:], T.up[:], T.us[:], ["us"], ["uq"])
+    copy("V", T.vq[:].bitcast(u32), T.uq[:].bitcast(u32).indirect(T.uoff[:]), ["uq", "uoff"], ["vq"])
+    copy("V", T.vp[:], T.up[:].indirect(T.uoff[:]), ["uq", "uoff"], ["vp"])
+
+    zk = ["z%d" % b for b in range(4)]
+    for t in range(R):
+        jv = JV[t]
+        ns = J - jv
+        o = 3 * (SMAX - ns)
+        zq, zp, zn = T["zq%d" % t], T["zp%d" % t], "zq%d" % t
+        quant(zq[:], zp[:], T.z[:], zk, [zn])
+        if t > 0:
+            copy("V", T.pp3[:, C + L * (t - 1):C + L * t], T[DB[3]][:, 0:L], [DB[3]], ["pp3"])
+        else:
+            ts(T.tpf[:], T.tops[:], float(UP - C), A.add, r=["tops"], w=["tpf"])
+        for b in AHEAD[t]:
+            gather_top(t, b)
+        mm("pb0", L, T.vq[:], T.vp[:], zq[:], zp[:], ["vq", "vp", zn])
+        for b in range(4):
+            mm("pb%d" % (2 + b), L, T.wq[:, 128 * b:128 * b + 128], T.wp[:, 128 * b:128 * b + 128], zq[:], zp[:], ["wq", "wp", zn])
+        mm("pb1", L, T.vq[:], T.vp[:], zq[:], zp[:], ["vq", "vp", zn])
+        s0, s1 = T.pb0, T.pb1
+        for b in range(4):
+            op("S", lambda e, b=b: e.activation(T.h[:, b:4 * L:4], T["pb%d" % (2 + b)][:, 0:L], F.Relu, scale=0.015625),
+               ["pb%d" % (2 + b)], ["h%d" % b])
+        tt(T.mk[:], s0[:, 0:L], T.mask[:], A.mult, ["pb0", "mask"], ["mk"])
+        if t > 0:
+            ts(T.tpf[:], T.held[:, last], T.cols[:, 0:1], A.add, float(UP - C - L * t), A.add, r=["held", "colv"], w=["tpf"])
+        scan(T.hold[:], T.keep[:], T.mk[:], 0.0, A.mult, A.add, ["keep", "mk"], ["hold"])
+
+        def compare(j):
+            nb, own, base = 16 * j + 16, T.hold[:, 16 * j + 15:16 * j + 16], L * j
+            ts(T.cmp[:, base:base + nb], s0[:, 0:nb], own, A.is_ge, r=["pb0", "hold"], w=["ca%d" % j])
+            ts(T.cmp[:, base + nb:base + L], s0[:, nb:L], own, A.is_gt, r=["pb0", "hold"], w=["cb%d" % j])
+
+        def total(j):
+            base = L * j
+            scan(T.cnt[:, hl * j:hl * j + hl], T.cmp[:, base:base + hl], T.cmp[:, base + hl:base + L], T.cc[:, j:j + 1],
+                 A.add, A.add, ["ca%d" % j, "cb%d" % j, "cc"], ["cnt%d" % j])
+
+        def sign(k):
+            j, base = jv + k, L * k
+            op("S", lambda e: e.activation(T.sgn[:, base:base + L], s1[:, 0:L], F.Sign,
+                                           bias=T.hold[:, 16 * j + 15:16 * j + 16], scale=-1.0),
+               ["pb1", "hold"], ["sa%d" % k, "sb%d" % k])
+
+        def sign_total(k):
+            nb, base, at = 16 * (jv + k) + 16, L * k, o + 3 * k
+            v = T.sgn[:, base:base + nb]
+            op("S", lambda e: e.activation(v, v, F.Sign, bias=0.5, scale=-1.0, accum_out=T.ab[:, at + 1:at + 2]),
+               ["sa%d" % k, "ab"], ["sa%d" % k, "aba%d" % (jv + k)])
+            if nb < L:
+                v2 = T.sgn[:, base + nb:base + L]
+                op("S", lambda e: e.activation(v2, v2, F.Sign, bias=-0.5, scale=-1.0, accum_out=T.ab[:, at + 2:at + 3]),
+                   ["sb%d" % k, "ab"], ["sb%d" % k, "abb%d" % (jv + k)])
+
+        new = slice(C + L * t, C + L * t + L)
+
+        def new_sum(b):
+            tt(T["sp%d" % b][:, new], T[DB[b]][:, 0:L], T.a0[:, L * b:L * b + L], A.add, [DB[b], "a0%d" % b], ["sp%d" % b])
+
+        def new_nodes(b):
+            copy("S", T["pp%d" % b][:, new], T[DB[b]][:, 0:L], [DB[b]], ["pp%d" % b])
+
+        ts(T.la[:], T.hold[:, last], 0.0, A.is_lt, 2 * STEP, A.mult, r=["hold"], w=["la"])
+        tt(T.same[:], s0[:, 0:L], T.hold[:], A.is_equal, ["pb0", "hold"], ["same"])
+        compare(0)
+        tt(T.lb[:], T.la[:], T.lane[:], A.add, ["la", "lane"], ["lb"])
+        scan(T.cq[:], T.keep[:], T.same[:], 0.0, A.mult, A.add, ["keep", "same"], ["cq"])
+        compare(1)
+        hq, hp = T["hq%d" % t], T["hp%d" % t]
+        quant(hq[:], hp[:], T.h[:], ["h%d" % b for b in range(4)], ["hq%d" % t])
+        lq, lp, arr = T["lq%d" % t], T["lp%d" % t], T.sem["arr%d" % t]
+        remote(lambda: g.remote_dma(lq[:].bitcast(u8), hq[:].bitcast(u8), arr, T.sem.sent, pid, rid, engines), n_out, ["hq%d" % t])
+        remote(lambda: g.remote_dma(lp[:], hp[:], arr, T.sem.sent, pid, rid, engines), n_out, ["hq%d" % t])
+        arrival("arr%d" % t, 2 * n_in, "land%d" % t)
+        if t == 0:
+            count_up(T.tb[:, ROW[1]:ROW[R] + L], R * L, 0, ["row%d" % k for k in range(1, R + 1)])
+        for b in range(4):
+            mm(DB[b], L, T.eq[:, 128 * b:128 * b + 128], T.ep[:, 128 * b:128 * b + 128], lq[:], lp[:],
+               ["eq%d" % b, "land%d" % t])
+        tt(T.lc[:], T.lb[:], T.tpf[:], A.min, ["lb", "tpf"], ["lc"])
+        ts(T.cc[:], T.cq[:, last], -1.0, A.mult, -float(hl), A.add, r=["cq"], w=["cc"])
+        ts(T.ab[:, o:3 * SMAX:3], T.cq[:, 16 * jv + 15:L:16], -2.0, A.mult, r=["cq", "ab"], w=["abc"])
+        ts(T.noff[:], T.lc[:], float(C + L * t), A.add, r=["lc"], w=["noff"])
+        sign(0)
+        for k in range(1, ns):
+            sign(k)
+            sign_total(k - 1)
+        copy("S", T.nrow[:], T.tb[:, 0:ROW[t]].indirect(T.noff[:]),
+             ["tb0", "tb1", "par", "noff"] + ["row%d" % k for k in range(t)], ["nrow"])
+        sign_total(ns - 1)
+        total(0)
+        for j in range(2, jv):
+            compare(j)
+            total(j - 1)
+        total(jv - 1)
+        scan(T.ab2[:, 0:3 * ns], T.keep3[:, 0:3 * ns], T.ab[:, o:3 * SMAX], 0.0, A.mult, A.add,
+             ["keep3", "abc", "ab"] + ["aba%d" % k for k in range(jv, J)] + ["abb%d" % k for k in range(jv, J)], ["ab2"])
+        ts(T.roff[:, 0:jv], T.cnt[:, hl - 1:hl * jv:hl], float(hl), A.add, r=["cnt%d" % j for j in range(jv)], w=["roffv"])
+        ts(T.roff[:, jv:J], T.ab2[:, 2:3 * ns:3], 0.5, A.mult, float(hl), A.add, r=["ab2"], w=["roffs"])
+        if t == R - 1:
+            for b in range(4):
+                gather_top(t, b)
+        else:
+            if t == 0:
+                copy("S", T.tb[:, ROW[0]:ROW[0] + L], T.tb[:, 0:C].indirect(T.toff0[:]), ["tb0", "toff0"], ["row0"])
+            else:
+                gather_top(t, 2)
+            gather_top(t, 3)
+            new_nodes(1)
+            new_nodes(2)
+        row, rk = T.tb[:, ROW[t + 1]:ROW[t + 1] + L], "row%d" % (t + 1)
+        copy("V", row.indirect(T.roff[:]), T.nrow[:], ["nrow", "roffv", "roffs"], [rk])
+        new_sum(0)
+        if t < R - 1:
+            new_nodes(0)
+        scan(T.held[:], T.kmin[:], row, 0.0, A.add, A.min, ["kmin", rk], ["held"])
+        ts(T["toff%d" % (t + 1)][:], T.held[:, last], T.cols[:, 0:1], A.add, r=["held", "colv"], w=["toff%d" % (t + 1)])
+        if t == R - 1:
+            dma("Y", T.ol[:], T.tb[0:128:16, ROW[R]:ROW[R] + L], [rk], [])
+        for b in range(1, 4):
+            new_sum(b)
+        for b in range(4):
+            gather_z("S" if b < 3 else "V", t + 1, b)
+
+    zq, zp, zn = T["zq%d" % R], T["zp%d" % R], "zq%d" % R
+    quant(zq[:], zp[:], T.z[:], zk, [zn])
+    mm("pb0", hl, T.uq[:], T.up[:], zq[:, 0:hl], zp[:, 0:hl], ["uq", zn])
+    mm("pb1", hl, T.uq[:], T.up[:], zq[:, hl:L], zp[:, hl:L], ["uq", zn])
+    dma("Y", T.oc[:], zq[:].bitcast(u8), [zn], [])
+    for k in range(4):
+        dma("YS"[k % 2], T.osc[4 * k:4 * k + 4, :], zp[32 * k:32 * k + 4, :], [zn], [])
+    copy("V", T.ya[:], T.pb0[:, 0:hl], ["pb0"], ["ya"])
+    copy("S", T.yb[:], T.pb1[:, 0:hl], ["pb1"], ["yb"])
+    dma("Y", T.y[:, 0:hl], T.ya[:], ["ya"], [])
+    dma("S", T.y[:, hl:L], T.yb[:], ["yb"], [])
+    finish("G")

@@ -6,7 +6,7 @@ C, L, R = 512, 384, 3
 J = L // 16
 NODES = C + R * L
 JV = (15, 15, 15)
-AHEAD = ((1, 2), (0, 1), ())
+AHEAD = ((1, 2), (0, 1), (0,))
 DB = ("pb2", "pb3", "pb4", "pb6")
 JMAX = max(JV)
 SMAX = J - min(JV)
@@ -28,16 +28,15 @@ SCRATCH = {
     "itp": ("sbuf", [128, L], "int32"), "res": ("sbuf", [128, L], "int32"), "i16": ("sbuf", [128, J], "int32"),
     "mask": ("sbuf", [128, L], "bfloat16"), "keep": ("sbuf", [128, L], "bfloat16"), "kmin": ("sbuf", [128, L], "bfloat16"),
     "keep3": ("sbuf", [128, 3 * SMAX], "float32"), "cols": ("sbuf", [128, 8], "float32"),
-    "lane": ("sbuf", [128, J], "float32"),
+    "pk0": ("sbuf", [128, 2 * J], "float32"), "pk1": ("sbuf", [128, 2 * J], "float32"),
+    "pk2": ("sbuf", [128, 2 * J], "float32"),
     "uoff": ("sbuf", [128, 8], "uint16"), "po1": ("sbuf", [128, 32], "uint16"),
     "noff": ("sbuf", [128, J], "uint16"), "roff": ("sbuf", [128, J], "uint16"),
-    "tpf": ("sbuf", [128, J], "float32"), "la": ("sbuf", [128, J], "float32"), "lb": ("sbuf", [128, J], "float32"),
-    "lc": ("sbuf", [128, J], "float32"), "cc": ("sbuf", [128, J], "float32"),
     "mk": ("sbuf", [128, L], "float32"), "hold": ("sbuf", [128, L], "float32"),
     "same": ("sbuf", [128, L], "bfloat16"), "cq": ("sbuf", [128, L], "bfloat16"),
-    "cmp": ("sbuf", [128, L * JMAX], "bfloat16"), "cnt": ("sbuf", [128, (L // 2) * JMAX], "bfloat16"),
+    "cmp": ("sbuf", [128, L * JMAX], "bfloat16"), "cnt": ("sbuf", [128, (L // 2) * J], "bfloat16"),
     "sgn": ("sbuf", [128, L * SMAX], "bfloat16"),
-    "ab": ("sbuf", [128, 3 * SMAX], "float32"), "ab2": ("sbuf", [128, 3 * SMAX], "float32"),
+    "ab": ("sbuf", [128, 3 * SMAX], "float32"),
     "nrow": ("sbuf", [128, L], "float32"), "held": ("sbuf", [128, L], "float32"),
     "ya": ("sbuf", [128, L // 2], "float32"), "yb": ("sbuf", [128, L // 2], "float32"),
 }
@@ -91,7 +90,7 @@ def orderer(g, T):
         wait(q, marks)
 
     def after(q, sem, n, reads, writes):
-        count[sem] = count.get(sem, 0) + n
+        count[sem] = count.pop(sem, 0) + n
         mark = (sem, count[sem])
         clock[mark] = dict(known[q])
         clock[mark][sem] = count[sem]
@@ -124,7 +123,8 @@ def orderer(g, T):
         writer[key] = (sem, n)
 
     def finish(q):
-        wait(q, list(count.items()))
+        for mark in list(count.items()):
+            wait(q, [mark])
 
     return op, dma, remote, arrival, finish
 
@@ -183,7 +183,9 @@ def rank_program(g, core, T, topo):
     op("V", lambda e: e.memset(T.et[:], 0.0), [], ["et"])
     op("V", lambda e: e.memset(T.keep3[:], 1.0), [], ["keep3"])
     op("V", lambda e: e.memset(T.ab[:], 0.0), [], ["ab"])
+    op("V", lambda e: e.memset(T.pk0[:], 2 * STEP), [], ["la"])
     ts(T.keep3[:, 0:3 * SMAX:3], T.keep3[:, 0:3 * SMAX:3], 0.0, A.mult, r=["keep3"], w=["keep3"])
+    ts(T.keep3[:, 2:3 * SMAX:3], T.keep3[:, 2:3 * SMAX:3], 0.5, A.mult, r=["keep3"], w=["keep3"])
     ts(T.res[:], T.itp[:], 15, A.bitwise_and, r=["itp"], w=["res"])
     ts(T.et[:, 3:515:4], T.itp[:, 0:128], 128.0, A.is_equal, r=["itp", "et"], w=["et"])
     ts(T.mask[:], T.res[:], 0.0, A.is_equal, r=["res"], w=["mask"])
@@ -192,7 +194,7 @@ def rank_program(g, core, T, topo):
     copy("V", T.uoff[:], T.i16[:, 0:8], ["i16"], ["uoff"])
     op("S", lambda e: e.activation(T.keep[:], T.mask[:], F.Identity, bias=1.0, scale=-1.0), ["mask"], ["keep"])
     op("S", lambda e: e.activation(T.kmin[:], T.mask[:], F.Identity, bias=-STEP, scale=18 * STEP), ["mask"], ["kmin"])
-    ts(T.lane[:], T.i16[:], T.cols[:, 1:2], A.add, r=["i16", "colp"], w=["lane"])
+    ts(T.pk1[:, 0:2 * J:2], T.i16[:], T.cols[:, 1:2], A.add, r=["i16", "colp"], w=["lane"])
     copy("V", T.po1[:], T.pars[:], ["pars"], ["po1"])
     for b in range(4):
         quant(T.eq[:, 128 * b:128 * b + 128], T.ep[:, 128 * b:128 * b + 128], T.et[:, 3 - b:515 - b], ["et"], ["eq%d" % b])
@@ -201,6 +203,11 @@ def rank_program(g, core, T, topo):
     def gather_z(q, t, b):
         copy(q, T.z[:, b:4 * L:4], T["sp%d" % b][:, 0:C + L * t].indirect(T["toff%d" % t][:]),
              ["sp%d" % b, "toff%d" % t], ["z%d" % b])
+
+    def gather_half(q, t, b, k):
+        copy(q, T.z[:, 4 * hl * k + b:4 * hl * (k + 1):4],
+             T["sp%d" % b][:, 0:C + L * t].indirect(T["toff%d" % t][:, J // 2 * k:J // 2 * (k + 1)]),
+             ["sp%d" % b, "toff%d" % t, "z%d" % b], ["zh%d%d" % (b, k)])
 
     def gather_top(t, b):
         copy("S", T.a0[:, L * b:L * b + L], T["pp%d" % b][:, 0:C + L * t].indirect(T["toff%d" % t][:]),
@@ -218,12 +225,17 @@ def rank_program(g, core, T, topo):
            ["xs", "po1", "pp%d" % b], ["sp%d" % b])
         if b == 0:
             gather_top(0, b)
-        gather_z("S", 0, b)
-    quant(T.uq[:], T.up[:], T.us[:], ["us"], ["uq"])
+        if b == 1:
+            quant(T.uq[:], T.up[:], T.us[:], ["us"], ["uq"])
+        if b < 3:
+            gather_z("S", 0, b)
+        if b == 1:
+            copy("S", T.vp[:], T.up[:].indirect(T.uoff[:]), ["uq", "uoff"], ["vp"])
+    gather_half("V", 0, 3, 0)
+    gather_half("S", 0, 3, 1)
     copy("V", T.vq[:].bitcast(u32), T.uq[:].bitcast(u32).indirect(T.uoff[:]), ["uq", "uoff"], ["vq"])
-    copy("V", T.vp[:], T.up[:].indirect(T.uoff[:]), ["uq", "uoff"], ["vp"])
 
-    zk = ["z%d" % b for b in range(4)]
+    zk = ["z%d" % b for b in range(4)] + ["zh30", "zh31"]
     for t in range(R):
         jv = JV[t]
         ns = J - jv
@@ -233,7 +245,7 @@ def rank_program(g, core, T, topo):
         if t > 0:
             copy("V", T.pp3[:, C + L * (t - 1):C + L * t], T[DB[3]][:, 0:L], [DB[3]], ["pp3"])
         else:
-            ts(T.tpf[:], T.tops[:], float(UP - C), A.add, r=["tops"], w=["tpf"])
+            ts(T.pk1[:, 1:2 * J:2], T.tops[:], float(UP - C), A.add, r=["tops"], w=["tpf"])
         for b in AHEAD[t]:
             gather_top(t, b)
         mm("pb0", L, T.vq[:], T.vp[:], zq[:], zp[:], ["vq", "vp", zn])
@@ -246,18 +258,19 @@ def rank_program(g, core, T, topo):
                ["pb%d" % (2 + b)], ["h%d" % b])
         tt(T.mk[:], s0[:, 0:L], T.mask[:], A.mult, ["pb0", "mask"], ["mk"])
         if t > 0:
-            ts(T.tpf[:], T.held[:, last], T.cols[:, 0:1], A.add, float(UP - C - L * t), A.add, r=["held", "colv"], w=["tpf"])
+            ts(T.pk1[:, 1:2 * J:2], T.held[:, last], T.cols[:, 0:1], A.add, float(UP - C - L * t), A.add,
+               r=["held", "colv"], w=["tpf"])
         scan(T.hold[:], T.keep[:], T.mk[:], 0.0, A.mult, A.add, ["keep", "mk"], ["hold"])
 
         def compare(j):
             nb, own, base = 16 * j + 16, T.hold[:, 16 * j + 15:16 * j + 16], L * j
-            ts(T.cmp[:, base:base + nb], s0[:, 0:nb], own, A.is_ge, r=["pb0", "hold"], w=["ca%d" % j])
-            ts(T.cmp[:, base + nb:base + L], s0[:, nb:L], own, A.is_gt, r=["pb0", "hold"], w=["cb%d" % j])
+            ts(T.cmp[:, base:base + nb], s0[:, 0:nb], own, A.is_ge, -0.5, A.add, r=["pb0", "hold"], w=["ca%d" % j])
+            ts(T.cmp[:, base + nb:base + L], s0[:, nb:L], own, A.is_gt, -0.5, A.add, r=["pb0", "hold"], w=["cb%d" % j])
 
         def total(j):
             base = L * j
-            scan(T.cnt[:, hl * j:hl * j + hl], T.cmp[:, base:base + hl], T.cmp[:, base + hl:base + L], T.cc[:, j:j + 1],
-                 A.add, A.add, ["ca%d" % j, "cb%d" % j, "cc"], ["cnt%d" % j])
+            scan(T.cnt[:, hl * j:hl * j + hl], T.cmp[:, base:base + hl], T.cmp[:, base + hl:base + L],
+                 T.cq[:, 16 * j + 15:16 * j + 16], A.add, A.add, ["ca%d" % j, "cb%d" % j, "cq"], ["cnt%d" % j])
 
         def sign(k):
             j, base = jv + k, L * k
@@ -268,11 +281,11 @@ def rank_program(g, core, T, topo):
         def sign_total(k):
             nb, base, at = 16 * (jv + k) + 16, L * k, o + 3 * k
             v = T.sgn[:, base:base + nb]
-            op("S", lambda e: e.activation(v, v, F.Sign, bias=0.5, scale=-1.0, accum_out=T.ab[:, at + 1:at + 2]),
+            op("S", lambda e: e.activation(v, v, F.Sign, bias=0.5, scale=-1.0, accum_out=T.ab[:, at:at + 1]),
                ["sa%d" % k, "ab"], ["sa%d" % k, "aba%d" % (jv + k)])
             if nb < L:
                 v2 = T.sgn[:, base + nb:base + L]
-                op("S", lambda e: e.activation(v2, v2, F.Sign, bias=-0.5, scale=-1.0, accum_out=T.ab[:, at + 2:at + 3]),
+                op("S", lambda e: e.activation(v2, v2, F.Sign, bias=-0.5, scale=-1.0, accum_out=T.ab[:, at + 1:at + 2]),
                    ["sb%d" % k, "ab"], ["sb%d" % k, "abb%d" % (jv + k)])
 
         new = slice(C + L * t, C + L * t + L)
@@ -283,11 +296,11 @@ def rank_program(g, core, T, topo):
         def new_nodes(b):
             copy("S", T["pp%d" % b][:, new], T[DB[b]][:, 0:L], [DB[b]], ["pp%d" % b])
 
-        ts(T.la[:], T.hold[:, last], 0.0, A.is_lt, 2 * STEP, A.mult, r=["hold"], w=["la"])
+        ts(T.pk0[:, 1:2 * J:2], T.hold[:, last], 0.0, A.is_lt, 2 * STEP, A.mult, r=["hold"], w=["la"])
         tt(T.same[:], s0[:, 0:L], T.hold[:], A.is_equal, ["pb0", "hold"], ["same"])
         compare(0)
-        tt(T.lb[:], T.la[:], T.lane[:], A.add, ["la", "lane"], ["lb"])
-        scan(T.cq[:], T.keep[:], T.same[:], 0.0, A.mult, A.add, ["keep", "same"], ["cq"])
+        scan(T.pk2[:], T.pk0[:], T.pk1[:], 0.0, A.add, A.min, ["la", "lane", "tpf"], ["lc"])
+        scan(T.cq[:], T.keep[:], T.same[:], 0.0, A.mult, A.subtract, ["keep", "same"], ["cq"])
         compare(1)
         hq, hp = T["hq%d" % t], T["hp%d" % t]
         quant(hq[:], hp[:], T.h[:], ["h%d" % b for b in range(4)], ["hq%d" % t])
@@ -300,10 +313,8 @@ def rank_program(g, core, T, topo):
         for b in range(4):
             mm(DB[b], L, T.eq[:, 128 * b:128 * b + 128], T.ep[:, 128 * b:128 * b + 128], lq[:], lp[:],
                ["eq%d" % b, "land%d" % t])
-        tt(T.lc[:], T.lb[:], T.tpf[:], A.min, ["lb", "tpf"], ["lc"])
-        ts(T.cc[:], T.cq[:, last], -1.0, A.mult, -float(hl), A.add, r=["cq"], w=["cc"])
-        ts(T.ab[:, o:3 * SMAX:3], T.cq[:, 16 * jv + 15:L:16], -2.0, A.mult, r=["cq", "ab"], w=["abc"])
-        ts(T.noff[:], T.lc[:], float(C + L * t), A.add, r=["lc"], w=["noff"])
+        copy("V", T.ab[:, o + 2:3 * SMAX:3], T.cq[:, 16 * jv + 15:L:16], ["cq", "ab"], ["abc"])
+        ts(T.noff[:], T.pk2[:, 1:2 * J:2], float(C + L * t), A.add, r=["lc"], w=["noff"])
         sign(0)
         for k in range(1, ns):
             sign(k)
@@ -316,12 +327,12 @@ def rank_program(g, core, T, topo):
             compare(j)
             total(j - 1)
         total(jv - 1)
-        scan(T.ab2[:, 0:3 * ns], T.keep3[:, 0:3 * ns], T.ab[:, o:3 * SMAX], 0.0, A.mult, A.add,
-             ["keep3", "abc", "ab"] + ["aba%d" % k for k in range(jv, J)] + ["abb%d" % k for k in range(jv, J)], ["ab2"])
-        ts(T.roff[:, 0:jv], T.cnt[:, hl - 1:hl * jv:hl], float(hl), A.add, r=["cnt%d" % j for j in range(jv)], w=["roffv"])
-        ts(T.roff[:, jv:J], T.ab2[:, 2:3 * ns:3], 0.5, A.mult, float(hl), A.add, r=["ab2"], w=["roffs"])
+        scan(T.cnt[:, hl * jv + hl // 3 - 1:hl * J:hl // 3], T.keep3[:, 0:3 * ns], T.ab[:, o:3 * SMAX], 0.0, A.mult, A.add,
+             ["keep3", "abc", "ab"] + ["aba%d" % k for k in range(jv, J)] + ["abb%d" % k for k in range(jv, J)],
+             ["cnt%d" % k for k in range(jv, J)])
+        ts(T.roff[:], T.cnt[:, hl - 1:hl * J:hl], float(hl), A.add, r=["cnt%d" % j for j in range(J)], w=["roff"])
         if t == R - 1:
-            for b in range(4):
+            for b in range(len(AHEAD[t]), 4):
                 gather_top(t, b)
         else:
             if t == 0:
@@ -332,7 +343,7 @@ def rank_program(g, core, T, topo):
             new_nodes(1)
             new_nodes(2)
         row, rk = T.tb[:, ROW[t + 1]:ROW[t + 1] + L], "row%d" % (t + 1)
-        copy("V", row.indirect(T.roff[:]), T.nrow[:], ["nrow", "roffv", "roffs"], [rk])
+        copy("V", row.indirect(T.roff[:]), T.nrow[:], ["nrow", "roff"], [rk])
         new_sum(0)
         if t < R - 1:
             new_nodes(0)
@@ -342,18 +353,23 @@ def rank_program(g, core, T, topo):
             dma("Y", T.ol[:], T.tb[0:128:16, ROW[R]:ROW[R] + L], [rk], [])
         for b in range(1, 4):
             new_sum(b)
-        for b in range(4):
-            gather_z("S" if b < 3 else "V", t + 1, b)
+        if t < R - 1:
+            for b in range(4):
+                gather_z("S" if b < 3 else "V", t + 1, b)
 
-    zq, zp, zn = T["zq%d" % R], T["zp%d" % R], "zq%d" % R
-    quant(zq[:], zp[:], T.z[:], zk, [zn])
-    mm("pb0", hl, T.uq[:], T.up[:], zq[:, 0:hl], zp[:, 0:hl], ["uq", zn])
-    mm("pb1", hl, T.uq[:], T.up[:], zq[:, hl:L], zp[:, hl:L], ["uq", zn])
-    dma("Y", T.oc[:], zq[:].bitcast(u8), [zn], [])
+    zq, zp = T["zq%d" % R], T["zp%d" % R]
+    for b, k in ((0, 0), (0, 1), (1, 0), (2, 0), (1, 1), (2, 1)):
+        gather_half("S", R, b, k)
+    for k in range(2):
+        cols, zn = slice(hl * k, hl * k + hl), "zq%d%d" % (R, k)
+        gather_half("V", R, 3, k)
+        quant(zq[:, cols], zp[:, cols], T.z[:, 4 * hl * k:4 * hl * (k + 1)], ["zh%d%d" % (b, k) for b in range(4)], [zn])
+        mm("pb%d" % k, hl, T.uq[:], T.up[:], zq[:, cols], zp[:, cols], ["uq", zn])
+        dma("Y", T.oc[:, 4 * hl * k:4 * hl * (k + 1)], zq[:, cols].bitcast(u8), [zn], [])
+    copy("S", T.ya[:], T.pb0[:, 0:hl], ["pb0"], ["ya"])
+    dma("S", T.y[:, 0:hl], T.ya[:], ["ya"], [])
+    copy("V", T.yb[:], T.pb1[:, 0:hl], ["pb1"], ["yb"])
     for k in range(4):
-        dma("YS"[k % 2], T.osc[4 * k:4 * k + 4, :], zp[32 * k:32 * k + 4, :], [zn], [])
-    copy("V", T.ya[:], T.pb0[:, 0:hl], ["pb0"], ["ya"])
-    copy("S", T.yb[:], T.pb1[:, 0:hl], ["pb1"], ["yb"])
-    dma("Y", T.y[:, 0:hl], T.ya[:], ["ya"], [])
-    dma("S", T.y[:, hl:L], T.yb[:], ["yb"], [])
+        dma("SY"[k // 2], T.osc[4 * k:4 * k + 4, :], zp[32 * k:32 * k + 4, :], ["zq%d0" % R, "zq%d1" % R], [])
+    dma("Y", T.y[:, hl:L], T.yb[:], ["yb"], [])
     finish("G")

@@ -4,15 +4,31 @@ A = AluOpType
 F = ActivationFunctionType
 C, L, R = 512, 384, 3
 J = L // 16
+JH, HL = J // 2, L // 2
 NODES = C + R * L
-JV = (15, 15, 15)
-AHEAD = ((1, 2), (0, 1), (0,))
+NA, NB = 3, 8
+FIRST = "i b y x0 k a S00 x1 x2 x3 S01 u S10 S11 S20 S21 S30 v p q0 S31".split()
+FRONT = "a1 a0 a2 a3 m0 q1 r0 o0 e0 m1 r1 c0 o1 r3 r2 C e1 H c1 L C C P C N C C C".split()
+END = ["n2 s1 g s0 h t s3 s2 N1 V30 n0 S10 S00 S20 S01 V31 S21 q0 N3 S11".split()] * 2 + [
+    "g s0 h t S00 s1 s3 S10 s2 V30 S20 V31 S11 S21 q0 S01".split()]
+ORDER = (
+    "0e0a000102030405060g0h0b0j0k0u0r070n08170i0v0l0s0m0x13090q0f0p0t0c0w160d0z101114120y151c18191e0o1a1h1g1b1d1i1j1k"
+    "1f1l1m1n1t1r1q1p1v1o1s1w1x1y1z201u21222324252627282d292r2a2c2e2f2b2g2h2i2j2k2l3f3b2q2s4e4b4d2t2z4h2u2x2p4i324g4n"
+    "3h3e433c463d3w3q3k3t3j3o3l3v3i413n3m3x3g332v2w3140483z3r493s4442473u3y3p45394a352y3836374c4f343a4l304k4j4p4m4r4o"
+    "4t4u4s4v4x4y4w4q515253545559582m575a502o5c5b4z2n5d5g5e5f5j5l5h5i5n5o5s5q5p5k5m565r5t5u6061625x635w645y655z666768"
+    "695v6a6b6c6g6f8f6i6e7d6k6l6m6r6p6n6o7l878377736w8h6j8i8k766d72796t8e7x7f6u7g716v6y807o7r7h6h7a7c7b75786z8r8n8g7p"
+    "7n7j8b8c887m7v7u7i7q847s867t8a8582897w7z7y818d7k8j708m6x8p747e8v8l8t8s8o8x8u8w8y8z908q919395969798999c9d9e926q9b"
+    "9f6s9a949g9h9j9k9m9l9n9y9q9o9i9r9p9s9t9w9v9ua4a5a69xa1a7a0a8a2a9a3aaabacad9zaeagalafaxahamb4aibcbbakajaoapaqatbl"
+    "bhc5c2btawbwbnbibrbsbpbzbyc9c3bkc0azancjb5b3bfb0bgb1avbmb8bactb9beayckcqcgb7bjcebobqc6c8cbcdccc7bvbxcabuc1cfc4bd"
+    "cicocpb6chcub2crclcmcycvcxcnczcwcsd2d1d0d3d5d4d6d7d8d9dadbdcdldfddardedgdqasdiaudjdkdmdodndhdrdsdtdpdudve2dwdxdy"
+    "e1dze0e3e4e5")
+SWAP = (42, 63, 194, 199, 209, 210, 211, 342, 348, 357, 359, 488, 502)
 DB = ("pb2", "pb3", "pb4", "pb6")
-JMAX = max(JV)
-SMAX = J - min(JV)
-UP = NODES
+UP = R * L
 ROW = [UP + C + L * t for t in range(R + 1)]
 STEP = 4096.0
+FREE = 2 ** 23
+WIN = L + 8
 
 SCRATCH = {
     "xs": ("sbuf", [128, 4 * C], "bfloat16"), "us": ("sbuf", [128, 512], "bfloat16"),
@@ -24,21 +40,22 @@ SCRATCH = {
     "eq": ("sbuf", [128, 512], "float8_e4m3fn_x4"), "ep": ("sbuf", [128, 512], "uint8"),
     "z": ("sbuf", [128, 4 * L], "bfloat16"), "h": ("sbuf", [128, 4 * L], "bfloat16"),
     "a0": ("sbuf", [128, 4 * L], "bfloat16"),
-    "tb": ("sbuf", [128, ROW[R] + L], "float32"),
-    "itp": ("sbuf", [128, L], "int32"), "res": ("sbuf", [128, L], "int32"), "i16": ("sbuf", [128, J], "int32"),
+    "tb": ("sbuf", [128, ROW[R] + L], "float32"), "idn": ("sbuf", [128, C], "float32"),
+    "wn": ("sbuf", [128, 2 * WIN * R], "float32"),
+    "itp": ("sbuf", [128, 128], "int32"), "res": ("sbuf", [128, 128], "int32"), "i16": ("sbuf", [128, J], "int32"),
     "mask": ("sbuf", [128, L], "bfloat16"), "keep": ("sbuf", [128, L], "bfloat16"), "kmin": ("sbuf", [128, L], "bfloat16"),
-    "keep3": ("sbuf", [128, 3 * SMAX], "float32"), "cols": ("sbuf", [128, 8], "float32"),
+    "kbig": ("sbuf", [128, L], "bfloat16"), "p2": ("sbuf", [128, L], "bfloat16"), "ph": ("sbuf", [128, L], "bfloat16"),
+    "keep3": ("sbuf", [128, 3 * JH], "float32"), "cols": ("sbuf", [128, 8], "float32"),
     "pk0": ("sbuf", [128, 2 * J], "float32"), "pk1": ("sbuf", [128, 2 * J], "float32"),
     "pk2": ("sbuf", [128, 2 * J], "float32"),
-    "uoff": ("sbuf", [128, 8], "uint16"), "po1": ("sbuf", [128, 32], "uint16"),
-    "noff": ("sbuf", [128, J], "uint16"), "roff": ("sbuf", [128, J], "uint16"),
+    "uoff": ("sbuf", [128, 8], "uint16"), "po": ("sbuf", [128, 32], "uint16"),
+    "noff": ("sbuf", [128, J], "uint16"), "roff": ("sbuf", [128, J], "uint16"), "moff": ("sbuf", [128, J], "uint16"),
     "mk": ("sbuf", [128, L], "float32"), "hold": ("sbuf", [128, L], "float32"),
     "same": ("sbuf", [128, L], "bfloat16"), "cq": ("sbuf", [128, L], "bfloat16"),
-    "cmp": ("sbuf", [128, L * JMAX], "bfloat16"), "cnt": ("sbuf", [128, (L // 2) * J], "bfloat16"),
-    "sgn": ("sbuf", [128, L * SMAX], "bfloat16"),
-    "ab": ("sbuf", [128, 3 * SMAX], "float32"),
+    "cmp": ("sbuf", [128, (L + HL) * JH], "bfloat16"), "cnt": ("sbuf", [128, (L + HL) * JH // 2], "bfloat16"),
+    "ab": ("sbuf", [128, 3 * J], "float32"),
     "nrow": ("sbuf", [128, L], "float32"), "held": ("sbuf", [128, L], "float32"),
-    "ya": ("sbuf", [128, L // 2], "float32"), "yb": ("sbuf", [128, L // 2], "float32"),
+    "ya": ("sbuf", [128, HL], "float32"), "yb": ("sbuf", [128, HL], "float32"),
 }
 for _b in range(4):
     SCRATCH["sp%d" % _b] = ("sbuf", [128, NODES], "bfloat16")
@@ -52,7 +69,7 @@ for _t in range(R):
         SCRATCH["%s%d" % (_n, _t)] = ("sbuf", [128, L], "float8_e4m3fn_x4")
     for _n in ("hp", "lp"):
         SCRATCH["%s%d" % (_n, _t)] = ("sbuf", [128, L], "uint8")
-for _b in range(7):
+for _b in range(8):
     SCRATCH["pb%d" % _b] = ("psum", [128, 512], "float32")
 
 NDMA = 16
@@ -63,7 +80,7 @@ def orderer(g, T):
     queue = {"V": g.vector, "S": g.scalar, "P": g.tensor, "G": g, "Y": g.sync}
     known = {q: {} for q in queue}
     count, clock, writer, readers = {}, {}, {}, {}
-    ndma = [0]
+    noted = []
 
     def wait(q, marks):
         need = {}
@@ -101,30 +118,42 @@ def orderer(g, T):
             readers[k] = []
 
     def op(q, call, reads, writes):
-        before(q, reads, writes)
-        call(queue[q]).then_inc(T.sem["s" + q], 1)
-        after(q, "s" + q, 1, reads, writes)
+        noted.append(["op", q, call, reads, writes])
 
     def dma(q, out, in_, reads, writes):
-        sem = "d%d" % ndma[0]
-        ndma[0] += 1
-        before(q, reads, writes)
-        queue[q].dma_start(out, in_).then_inc(T.sem[sem], 16)
-        after(q, sem, 16, reads, writes)
+        noted.append(["dma", q, (out, in_, "d%d" % sum(e[0] == "dma" for e in noted)), reads, writes])
 
     def remote(call, n, reads):
-        before("G", reads, [])
-        call()
-        after("G", "sent", n, [], [])
+        noted.append(["remote", "G", call, reads, n, None])
 
     def arrival(sem, n, key):
-        count[sem] = n
-        clock[(sem, n)] = {sem: n}
-        writer[key] = (sem, n)
+        noted[-1][5] = (sem, n, key)
 
-    def finish(q):
+    def finish(last):
+        for at in range(0, len(ORDER), 2):
+            i = int(ORDER[at:at + 2], 36)
+            kind, q, call, reads, writes = noted[i][:5]
+            if kind == "op":
+                if i in SWAP:
+                    q = "V" if q == "S" else "S"
+                before(q, reads, writes)
+                (call[q] if isinstance(call, dict) else call)(queue[q]).then_inc(T.sem["s" + q], 1)
+                after(q, "s" + q, 1, reads, writes)
+            elif kind == "dma":
+                before(q, reads, writes)
+                queue[q].dma_start(call[0], call[1]).then_inc(T.sem[call[2]], 16)
+                after(q, call[2], 16, reads, writes)
+            else:
+                before(q, reads, [])
+                call()
+                after(q, "sent", writes, [], [])
+                if noted[i][5]:
+                    sem, n, key = noted[i][5]
+                    count[sem] = n
+                    clock[(sem, n)] = {sem: n}
+                    writer[key] = (sem, n)
         for mark in list(count.items()):
-            wait(q, [mark])
+            wait(last, [mark])
 
     return op, dma, remote, arrival, finish
 
@@ -141,7 +170,15 @@ def rank_program(g, core, T, topo):
     op, dma, remote, arrival, finish = orderer(g, T)
     u8, u32 = dt.uint8, dt.uint32
     last = slice(15, L, 16)
-    hl = L // 2
+    half = (slice(0, HL), slice(HL, L))
+    lists = (slice(0, JH), slice(JH, J))
+    masks = ["mask%d" % k for k in range(L // 128)]
+
+    def both(key):
+        return [key + "0", key + "1"]
+
+    def fill(out, value, w):
+        op("V", lambda e: e.memset(out, value), [], w)
 
     def ts(out, in0, s1, o0, s2=None, o1=None, r=(), w=()):
         if o1 is None:
@@ -156,10 +193,11 @@ def rank_program(g, core, T, topo):
         op("V", lambda e: e.tensor_tensor_scan(out, d0, d1, init, o0, o1), r, w)
 
     def copy(q, out, in_, r, w):
-        if q == "V":
-            op("V", lambda e: e.tensor_copy(out, in_), r, w)
-        else:
-            op("S", lambda e: e.activation(out, in_, F.Copy), r, w)
+        op(q, {"V": lambda e: e.tensor_copy(out, in_), "S": lambda e: e.activation(out, in_, F.Copy)}, r, w)
+
+    def affine(q, out, in_, scale, bias, r, w):
+        op(q, {"V": lambda e: e.tensor_scalar(out, in_, scale, bias, A.mult, A.add),
+               "S": lambda e: e.activation(out, in_, F.Identity, bias=bias, scale=scale)}, r, w)
 
     def quant(out, scales, in_, r, w):
         op("V", lambda e: e.quantize_mx(out, scales, in_), r, w)
@@ -167,209 +205,275 @@ def rank_program(g, core, T, topo):
     def mm(bank, cols, lq, lp, rq, rp, r):
         op("P", lambda e: e.matmul_mx(T[bank][:, 0:cols], lq, lp, rq, rp, True, True), r, [bank])
 
-    def count_up(out, cols, base, w):
-        op("G", lambda e: e.iota(out, [[1, cols]], base, 0, allow_small_or_imprecise_dtypes=True), [], w)
+    def count_up(out, cols, base, step, w):
+        op("G", lambda e: e.iota(out, [[step, cols]], base, 0, allow_small_or_imprecise_dtypes=True), [], w)
+
+    def free_places(t):
+        count_up(T.wn[:, 2 * WIN * t:2 * WIN * (t + 1)], 2 * WIN, FREE, 0, ["wa%d" % t, "wb%d" % t])
+
+    def new_numbers(t):
+        count_up(T.tb[:, UP - L * (t + 1):UP - L * t], L, C + L * t, 1, ["new%d" % t])
 
     dma("S", T.pars[:], T.par[:], [], ["pars"])
-    dma("Y", T.xs[:], T.x[:], [], ["xs"])
     dma("Y", T.tops[:], T.top[:], [], ["tops"])
+    dma("Y", T.xs[:], T.x[:], [], ["xs"])
     dma("Y", T.us[:], T.u[:], [], ["us"])
     dma("Y", T.wq[:].bitcast(u8), T.wc[:], [], ["wq"])
     dma("Y", T.wp[:], T.ws[:], [], ["wp"])
 
-    op("G", lambda e: e.iota(T.itp[:], [[1, L]], 128, -1), [], ["itp"])
+    op("G", lambda e: e.iota(T.itp[:], [[1, 128]], 128, -1), [], ["itp"])
     op("G", lambda e: e.iota(T.i16[:], [[16, J]], 0, 0), [], ["i16"])
-    count_up(T.tb[:, 0:C], C, 0, ["tb0"])
-    op("V", lambda e: e.memset(T.et[:], 0.0), [], ["et"])
-    op("V", lambda e: e.memset(T.keep3[:], 1.0), [], ["keep3"])
-    op("V", lambda e: e.memset(T.ab[:], 0.0), [], ["ab"])
-    op("V", lambda e: e.memset(T.pk0[:], 2 * STEP), [], ["la"])
-    ts(T.keep3[:, 0:3 * SMAX:3], T.keep3[:, 0:3 * SMAX:3], 0.0, A.mult, r=["keep3"], w=["keep3"])
-    ts(T.keep3[:, 2:3 * SMAX:3], T.keep3[:, 2:3 * SMAX:3], 0.5, A.mult, r=["keep3"], w=["keep3"])
+    count_up(T.idn[:], C, 0, 1, ["idn"])
+    free_places(0)
+    fill(T.et[:], 0.0, ["et"])
+    for k, v in enumerate((0.0, 1.0, 0.5)):
+        fill(T.keep3[:, k:3 * JH:3], v, ["keep3%d" % k])
+    fill(T.pk0[:], 0.0, ["la"])
+    fill(T.ab[:, 3 * J - 2:3 * J - 1], 0.0, ["abb%d" % (J - 1)])
     ts(T.res[:], T.itp[:], 15, A.bitwise_and, r=["itp"], w=["res"])
     ts(T.et[:, 3:515:4], T.itp[:, 0:128], 128.0, A.is_equal, r=["itp", "et"], w=["et"])
-    ts(T.mask[:], T.res[:], 0.0, A.is_equal, r=["res"], w=["mask"])
+    for k in range(L // 128):
+        ts(T.mask[:, 128 * k:128 * k + 128], T.res[:], 0.0, A.is_equal, r=["res"], w=[masks[k]])
     ts(T.cols[:, 0:1], T.res[:, 15:16], STEP, A.mult, r=["res"], w=["colv"])
     ts(T.cols[:, 1:2], T.res[:, 15:16], -1.0, A.mult, 15.0, A.add, r=["res"], w=["colp"])
     copy("V", T.uoff[:], T.i16[:, 0:8], ["i16"], ["uoff"])
-    op("S", lambda e: e.activation(T.keep[:], T.mask[:], F.Identity, bias=1.0, scale=-1.0), ["mask"], ["keep"])
-    op("S", lambda e: e.activation(T.kmin[:], T.mask[:], F.Identity, bias=-STEP, scale=18 * STEP), ["mask"], ["kmin"])
-    ts(T.pk1[:, 0:2 * J:2], T.i16[:], T.cols[:, 1:2], A.add, r=["i16", "colp"], w=["lane"])
-    copy("V", T.po1[:], T.pars[:], ["pars"], ["po1"])
+    affine("S", T.keep[:], T.mask[:], -1.0, 1.0, masks, ["keep"])
+    ts(T.cols[:, 4:4 + R], T.i16[:, 1:1 + R], L / 16.0, A.mult, T.cols[:, 0:1], A.add, r=["i16", "colv"], w=["colt"])
+    ts(T.pk1[:, 1:2 * J:2], T.i16[:], T.cols[:, 1:2], A.add, r=["i16", "colp"], w=["lane"])
+    copy("V", T.po[:], T.pars[:], ["pars"], ["po"])
+    copy("V", T.toff0[:], T.tops[:], ["tops"], both("toff0"))
+    ts(T.pk1[:, 0:2 * J:2], T.tops[:], float(L), A.add, r=["tops"], w=["tpf"])
     for b in range(4):
         quant(T.eq[:, 128 * b:128 * b + 128], T.ep[:, 128 * b:128 * b + 128], T.et[:, 3 - b:515 - b], ["et"], ["eq%d" % b])
-    copy("S", T.tb[:, UP:UP + C], T.tb[:, 0:C].indirect(T.po1[:]), ["tb0", "po1"], ["par"])
 
-    def gather_z(q, t, b):
-        copy(q, T.z[:, b:4 * L:4], T["sp%d" % b][:, 0:C + L * t].indirect(T["toff%d" % t][:]),
-             ["sp%d" % b, "toff%d" % t], ["z%d" % b])
-
-    def gather_half(q, t, b, k):
-        copy(q, T.z[:, 4 * hl * k + b:4 * hl * (k + 1):4],
-             T["sp%d" % b][:, 0:C + L * t].indirect(T["toff%d" % t][:, J // 2 * k:J // 2 * (k + 1)]),
-             ["sp%d" % b, "toff%d" % t, "z%d" % b], ["zh%d%d" % (b, k)])
+    def gather_z(q, t, b, k):
+        copy(q, T.z[:, 4 * HL * k + b:4 * HL * (k + 1):4], T["sp%d" % b][:, 0:C + L * t].indirect(T["toff%d" % t][:, lists[k]]),
+             ["sp%d" % b, "toff%d%d" % (t, k)], ["z%d%d" % (b, k)])
 
     def gather_top(t, b):
         copy("S", T.a0[:, L * b:L * b + L], T["pp%d" % b][:, 0:C + L * t].indirect(T["toff%d" % t][:]),
-             ["pp%d" % b, "toff%d" % t], ["a0%d" % b])
+             ["pp%d" % b] + both("toff%d" % t), ["a0%d" % b])
+
+    def layer(t, k):
+        for b in range(4):
+            mm("pb%d" % (2 + b), HL, T.wq[:, 128 * b:128 * b + 128], T.wp[:, 128 * b:128 * b + 128],
+               T["zq%d" % t][:, half[k]], T["zp%d" % t][:, half[k]], ["wq", "wp", "zq%d%d" % (t, k)])
+
+    def relu(b, k):
+        out, in_ = T.h[:, 4 * HL * k + b:4 * HL * (k + 1):4], T["pb%d" % (2 + b)][:, 0:HL]
+        op("S", {"V": lambda e: e.tensor_scalar(out, in_, 0.0, 0.015625, A.max, A.mult),
+                 "S": lambda e: e.activation(out, in_, F.Relu, scale=0.015625)}, ["pb%d" % (2 + b)], ["h%d%d" % (b, k)])
+
+    def quant_z(t, k):
+        zq, zp = T["zq%d" % t], T["zp%d" % t]
+        quant(zq[:, half[k]], zp[:, half[k]], T.z[:, 4 * HL * k:4 * HL * (k + 1)], ["z%d%d" % (b, k) for b in range(4)],
+              ["zq%d%d" % (t, k)])
+        if t == R:
+            mm("pb%d" % k, HL, T.uq[:], T.up[:], zq[:, half[k]], zp[:, half[k]], ["uq", "zq%d%d" % (t, k)])
+            dma("Y", T.oc[:, 4 * HL * k:4 * HL * (k + 1)], zq[:, half[k]].bitcast(u8), ["zq%d%d" % (t, k)], [])
+        elif k == 0:
+            mm("pb7", HL, T.vq[:], T.vp[:], zq[:, half[0]], zp[:, half[0]], ["vq", "vp", "zq%d0" % t])
+            layer(t, 0)
+        else:
+            zn = both("zq%d" % t)
+            mm("pb0", L, T.vq[:], T.vp[:], zq[:], zp[:], ["vq", "vp"] + zn)
+            layer(t, 1)
+            mm("pb1", L, T.vq[:], T.vp[:], zq[:], zp[:], ["vq", "vp"] + zn)
+
+    def read_step(t, s):
+        if s[0] in "SV":
+            gather_z(s[0], t, int(s[1]), int(s[2]))
+        else:
+            quant_z(t, int(s[1]))
 
     copy("V", T.pp0[:, 0:C], T.xs[:, 0:4 * C:4], ["xs"], ["pp0"])
-    copy("V", T.toff0[:], T.tops[:], ["tops"], ["toff0"])
-    copy("S", T.pp1[:, 0:C], T.xs[:, 1:4 * C:4], ["xs"], ["pp1"])
     for b in (2, 3):
         op("G", lambda e, b=b: e.affine_select(T["pp%d" % b][:, 0:C], T.xs[:, b:4 * C:4], [[1, C]], A.is_ge, 0.0, 0, 0),
            ["xs"], ["pp%d" % b])
-    count_up(T.tb[:, C:UP], UP - C, C, ["tb1"])
-    for b in range(4):
-        tt(T["sp%d" % b][:, 0:C], T["pp%d" % b][:, 0:C].indirect(T.po1[:]), T.xs[:, b:4 * C:4], A.add,
-           ["xs", "po1", "pp%d" % b], ["sp%d" % b])
-        if b == 0:
-            gather_top(0, b)
-        if b == 1:
+    new_numbers(0)
+    for s in FIRST:
+        if s[0] == "x":
+            b = int(s[1])
+            tt(T["sp%d" % b][:, 0:C], T["pp%d" % b][:, 0:C].indirect(T.po[:]), T.xs[:, b:4 * C:4], A.add,
+               ["xs", "po", "pp%d" % b], ["sp%d" % b])
+        elif s == "y":
+            copy("S", T.pp1[:, 0:C], T.xs[:, 1:4 * C:4], ["xs"], ["pp1"])
+        elif s == "i":
+            affine("S", T.kmin[:], T.mask[:], 18 * STEP, -STEP, masks, ["kmin"])
+        elif s == "k":
+            affine("S", T.kbig[:], T.mask[:], 1024.0 * FREE, 0.0, masks, ["kbig"])
+        elif s == "a":
+            copy("S", T.tb[:, UP:UP + C], T.idn[:].indirect(T.po[:]), ["idn", "po"], ["par"])
+        elif s == "b":
+            copy("S", T.tb[:, ROW[0]:ROW[0] + L], T.idn[:].indirect(T.toff0[:]), ["idn"] + both("toff0"), ["row0"])
+        elif s == "u":
             quant(T.uq[:], T.up[:], T.us[:], ["us"], ["uq"])
-        if b < 3:
-            gather_z("S", 0, b)
-        if b == 1:
+        elif s == "p":
             copy("S", T.vp[:], T.up[:].indirect(T.uoff[:]), ["uq", "uoff"], ["vp"])
-    gather_half("V", 0, 3, 0)
-    gather_half("S", 0, 3, 1)
-    copy("V", T.vq[:].bitcast(u32), T.uq[:].bitcast(u32).indirect(T.uoff[:]), ["uq", "uoff"], ["vq"])
-
-    zk = ["z%d" % b for b in range(4)] + ["zh30", "zh31"]
-    for t in range(R):
-        jv = JV[t]
-        ns = J - jv
-        o = 3 * (SMAX - ns)
-        zq, zp, zn = T["zq%d" % t], T["zp%d" % t], "zq%d" % t
-        quant(zq[:], zp[:], T.z[:], zk, [zn])
-        if t > 0:
-            copy("V", T.pp3[:, C + L * (t - 1):C + L * t], T[DB[3]][:, 0:L], [DB[3]], ["pp3"])
+        elif s == "v":
+            copy("V", T.vq[:].bitcast(u32), T.uq[:].bitcast(u32).indirect(T.uoff[:]), ["uq", "uoff"], ["vq"])
         else:
-            ts(T.pk1[:, 1:2 * J:2], T.tops[:], float(UP - C), A.add, r=["tops"], w=["tpf"])
-        for b in AHEAD[t]:
-            gather_top(t, b)
-        mm("pb0", L, T.vq[:], T.vp[:], zq[:], zp[:], ["vq", "vp", zn])
-        for b in range(4):
-            mm("pb%d" % (2 + b), L, T.wq[:, 128 * b:128 * b + 128], T.wp[:, 128 * b:128 * b + 128], zq[:], zp[:], ["wq", "wp", zn])
-        mm("pb1", L, T.vq[:], T.vp[:], zq[:], zp[:], ["vq", "vp", zn])
-        s0, s1 = T.pb0, T.pb1
-        for b in range(4):
-            op("S", lambda e, b=b: e.activation(T.h[:, b:4 * L:4], T["pb%d" % (2 + b)][:, 0:L], F.Relu, scale=0.015625),
-               ["pb%d" % (2 + b)], ["h%d" % b])
-        tt(T.mk[:], s0[:, 0:L], T.mask[:], A.mult, ["pb0", "mask"], ["mk"])
-        if t > 0:
-            ts(T.pk1[:, 1:2 * J:2], T.held[:, last], T.cols[:, 0:1], A.add, float(UP - C - L * t), A.add,
-               r=["held", "colv"], w=["tpf"])
-        scan(T.hold[:], T.keep[:], T.mk[:], 0.0, A.mult, A.add, ["keep", "mk"], ["hold"])
+            read_step(0, s)
 
-        def compare(j):
-            nb, own, base = 16 * j + 16, T.hold[:, 16 * j + 15:16 * j + 16], L * j
-            ts(T.cmp[:, base:base + nb], s0[:, 0:nb], own, A.is_ge, -0.5, A.add, r=["pb0", "hold"], w=["ca%d" % j])
-            ts(T.cmp[:, base + nb:base + L], s0[:, nb:L], own, A.is_gt, -0.5, A.add, r=["pb0", "hold"], w=["cb%d" % j])
+    s0, s1 = T.pb0, T.pb1
+    on_s = list(range(NA)) + list(range(J - NB, J))
+    on_v = [j for j in range(J) if j not in on_s]
 
-        def total(j):
-            base = L * j
-            scan(T.cnt[:, hl * j:hl * j + hl], T.cmp[:, base:base + hl], T.cmp[:, base + hl:base + L],
-                 T.cq[:, 16 * j + 15:16 * j + 16], A.add, A.add, ["ca%d" % j, "cb%d" % j, "cq"], ["cnt%d" % j])
+    def span(j):
+        lo = 0 if j < JH else HL
+        return lo, 16 * j + 16, (L * j if j < JH else L * JH + HL * (j - JH)) - lo
 
-        def sign(k):
-            j, base = jv + k, L * k
-            op("S", lambda e: e.activation(T.sgn[:, base:base + L], s1[:, 0:L], F.Sign,
-                                           bias=T.hold[:, 16 * j + 15:16 * j + 16], scale=-1.0),
-               ["pb1", "hold"], ["sa%d" % k, "sb%d" % k])
+    def compare(j):
+        lo, mid, base = span(j)
+        own, hk = T.hold[:, mid - 1:mid], "hold%d" % (j // JH)
+        ts(T.cmp[:, base + lo:base + mid], s0[:, lo:mid], own, A.is_ge, -0.5, A.add, r=["pb0", hk], w=["ca%d" % j])
+        ts(T.cmp[:, base + mid:base + L], s0[:, mid:L], own, A.is_gt, -0.5, A.add, r=["pb0", hk], w=["cb%d" % j])
 
-        def sign_total(k):
-            nb, base, at = 16 * (jv + k) + 16, L * k, o + 3 * k
-            v = T.sgn[:, base:base + nb]
-            op("S", lambda e: e.activation(v, v, F.Sign, bias=0.5, scale=-1.0, accum_out=T.ab[:, at:at + 1]),
-               ["sa%d" % k, "ab"], ["sa%d" % k, "aba%d" % (jv + k)])
-            if nb < L:
-                v2 = T.sgn[:, base + nb:base + L]
-                op("S", lambda e: e.activation(v2, v2, F.Sign, bias=-0.5, scale=-1.0, accum_out=T.ab[:, at + 1:at + 2]),
-                   ["sb%d" % k, "ab"], ["sb%d" % k, "abb%d" % (jv + k)])
+    def total(j):
+        lo, mid, base = span(j)
+        w, at = (L - lo) // 2, (base + lo) // 2
+        scan(T.cnt[:, at:at + w], T.cmp[:, 2 * at:2 * at + w], T.cmp[:, 2 * at + w:2 * at + 2 * w],
+             T.cq[:, mid - 1:mid], A.add, A.add, ["ca%d" % j, "cb%d" % j, "cq%d" % (j // JH)], ["cnt%d" % j])
 
-        new = slice(C + L * t, C + L * t + L)
+    def sign(j):
+        lo, mid, base = span(j)
+        op("S", lambda e: e.activation(T.cmp[:, base + lo:base + L], s1[:, lo:L], F.Sign,
+                                       bias=T.hold[:, mid - 1:mid], scale=-1.0),
+           ["pb1", "hold%d" % (j // JH)], ["ca%d" % j, "cb%d" % j])
 
-        def new_sum(b):
-            tt(T["sp%d" % b][:, new], T[DB[b]][:, 0:L], T.a0[:, L * b:L * b + L], A.add, [DB[b], "a0%d" % b], ["sp%d" % b])
+    def sign_total(j):
+        lo, mid, base = span(j)
+        v, v2 = T.cmp[:, base + lo:base + mid], T.cmp[:, base + mid:base + L]
+        op("S", lambda e: e.activation(v, v, F.Sign, bias=0.5, scale=-1.0, accum_out=T.ab[:, 3 * j:3 * j + 1]),
+           ["ca%d" % j], ["ca%d" % j, "aba%d" % j])
+        if mid < L:
+            op("S", lambda e: e.activation(v2, v2, F.Sign, bias=-0.5, scale=-1.0, accum_out=T.ab[:, 3 * j + 1:3 * j + 2]),
+               ["cb%d" % j], ["cb%d" % j, "abb%d" % j])
 
-        def new_nodes(b):
-            copy("S", T["pp%d" % b][:, new], T[DB[b]][:, 0:L], [DB[b]], ["pp%d" % b])
+    def join(j0, j1):
+        lo, _, base = span(j0)
+        at, third = (base + lo) // 2, (L - lo) // 6
+        scan(T.cnt[:, at + third - 1:at + 3 * third * (j1 - j0):third], T.keep3[:, 0:3 * (j1 - j0)], T.ab[:, 3 * j0:3 * j1],
+             0.0, A.mult, A.add,
+             ["keep30", "keep31", "keep32", "abc%d" % (j0 // JH)] + ["ab%s%d" % (c, j) for c in "ab" for j in range(j0, j1)],
+             ["cnt%d" % j for j in range(j0, j1)])
 
-        ts(T.pk0[:, 1:2 * J:2], T.hold[:, last], 0.0, A.is_lt, 2 * STEP, A.mult, r=["hold"], w=["la"])
-        tt(T.same[:], s0[:, 0:L], T.hold[:], A.is_equal, ["pb0", "hold"], ["same"])
-        compare(0)
-        scan(T.pk2[:], T.pk0[:], T.pk1[:], 0.0, A.add, A.min, ["la", "lane", "tpf"], ["lc"])
-        scan(T.cq[:], T.keep[:], T.same[:], 0.0, A.mult, A.subtract, ["keep", "same"], ["cq"])
-        compare(1)
-        hq, hp = T["hq%d" % t], T["hp%d" % t]
-        quant(hq[:], hp[:], T.h[:], ["h%d" % b for b in range(4)], ["hq%d" % t])
-        lq, lp, arr = T["lq%d" % t], T["lp%d" % t], T.sem["arr%d" % t]
+    def send_h(t):
+        hq, hp, lq, lp, arr = T["hq%d" % t], T["hp%d" % t], T["lq%d" % t], T["lp%d" % t], T.sem["arr%d" % t]
+        quant(hq[:], hp[:], T.h[:], ["h%d%d" % (b, k) for b in range(4) for k in range(2)], ["hq%d" % t])
         remote(lambda: g.remote_dma(lq[:].bitcast(u8), hq[:].bitcast(u8), arr, T.sem.sent, pid, rid, engines), n_out, ["hq%d" % t])
         remote(lambda: g.remote_dma(lp[:], hp[:], arr, T.sem.sent, pid, rid, engines), n_out, ["hq%d" % t])
         arrival("arr%d" % t, 2 * n_in, "land%d" % t)
-        if t == 0:
-            count_up(T.tb[:, ROW[1]:ROW[R] + L], R * L, 0, ["row%d" % k for k in range(1, R + 1)])
+        if t < R - 1:
+            free_places(t + 1)
+            new_numbers(t + 1)
         for b in range(4):
             mm(DB[b], L, T.eq[:, 128 * b:128 * b + 128], T.ep[:, 128 * b:128 * b + 128], lq[:], lp[:],
                ["eq%d" % b, "land%d" % t])
-        copy("V", T.ab[:, o + 2:3 * SMAX:3], T.cq[:, 16 * jv + 15:L:16], ["cq", "ab"], ["abc"])
-        ts(T.noff[:], T.pk2[:, 1:2 * J:2], float(C + L * t), A.add, r=["lc"], w=["noff"])
-        sign(0)
-        for k in range(1, ns):
-            sign(k)
-            sign_total(k - 1)
-        copy("S", T.nrow[:], T.tb[:, 0:ROW[t]].indirect(T.noff[:]),
-             ["tb0", "tb1", "par", "noff"] + ["row%d" % k for k in range(t)], ["nrow"])
-        sign_total(ns - 1)
-        total(0)
-        for j in range(2, jv):
-            compare(j)
-            total(j - 1)
-        total(jv - 1)
-        scan(T.cnt[:, hl * jv + hl // 3 - 1:hl * J:hl // 3], T.keep3[:, 0:3 * ns], T.ab[:, o:3 * SMAX], 0.0, A.mult, A.add,
-             ["keep3", "abc", "ab"] + ["aba%d" % k for k in range(jv, J)] + ["abb%d" % k for k in range(jv, J)],
-             ["cnt%d" % k for k in range(jv, J)])
-        ts(T.roff[:], T.cnt[:, hl - 1:hl * J:hl], float(hl), A.add, r=["cnt%d" % j for j in range(J)], w=["roff"])
-        if t == R - 1:
-            for b in range(len(AHEAD[t]), 4):
-                gather_top(t, b)
-        else:
-            if t == 0:
-                copy("S", T.tb[:, ROW[0]:ROW[0] + L], T.tb[:, 0:C].indirect(T.toff0[:]), ["tb0", "toff0"], ["row0"])
-            else:
-                gather_top(t, 2)
-            gather_top(t, 3)
-            new_nodes(1)
-            new_nodes(2)
-        row, rk = T.tb[:, ROW[t + 1]:ROW[t + 1] + L], "row%d" % (t + 1)
-        copy("V", row.indirect(T.roff[:]), T.nrow[:], ["nrow", "roff"], [rk])
-        new_sum(0)
-        if t < R - 1:
-            new_nodes(0)
-        scan(T.held[:], T.kmin[:], row, 0.0, A.add, A.min, ["kmin", rk], ["held"])
-        ts(T["toff%d" % (t + 1)][:], T.held[:, last], T.cols[:, 0:1], A.add, r=["held", "colv"], w=["toff%d" % (t + 1)])
-        if t == R - 1:
-            dma("Y", T.ol[:], T.tb[0:128:16, ROW[R]:ROW[R] + L], [rk], [])
-        for b in range(1, 4):
-            new_sum(b)
-        if t < R - 1:
-            for b in range(4):
-                gather_z("S" if b < 3 else "V", t + 1, b)
 
-    zq, zp = T["zq%d" % R], T["zp%d" % R]
-    for b, k in ((0, 0), (0, 1), (1, 0), (2, 0), (1, 1), (2, 1)):
-        gather_half("S", R, b, k)
-    for k in range(2):
-        cols, zn = slice(hl * k, hl * k + hl), "zq%d%d" % (R, k)
-        gather_half("V", R, 3, k)
-        quant(zq[:, cols], zp[:, cols], T.z[:, 4 * hl * k:4 * hl * (k + 1)], ["zh%d%d" % (b, k) for b in range(4)], [zn])
-        mm("pb%d" % k, hl, T.uq[:], T.up[:], zq[:, cols], zp[:, cols], ["uq", zn])
-        dma("Y", T.oc[:, 4 * hl * k:4 * hl * (k + 1)], zq[:, cols].bitcast(u8), [zn], [])
-    copy("S", T.ya[:], T.pb0[:, 0:hl], ["pb0"], ["ya"])
-    dma("S", T.y[:, 0:hl], T.ya[:], ["ya"], [])
-    copy("V", T.yb[:], T.pb1[:, 0:hl], ["pb1"], ["yb"])
+    for t in range(R):
+        if t > 0:
+            affine("S", T.pk1[:, 0:2 * J:2], T.held[:, last], 1.0, T.cols[:, 4 + t:5 + t], ["held", "colt"], ["tpf"])
+        done = 0
+        for s in FRONT:
+            k = int(s[1]) if len(s) > 1 else 0
+            bank, hs = ("pb7", "pb0")[k % 2], half[k % 2]
+            if s[0] == "q":
+                quant_z(t, k)
+            elif s[0] in "ar":
+                relu(k, "ar".index(s[0]))
+            elif s[0] == "m":
+                tt(T.mk[:, hs], T[bank][:, hs], T.mask[:, hs], A.mult, [bank] + masks, ["mk%d" % k])
+            elif s[0] == "o":
+                scan(T.hold[:, hs], T.keep[:, hs], T.mk[:, hs], 0.0, A.mult, A.add, ["keep", "mk%d" % k], ["hold%d" % k])
+            elif s[0] == "e":
+                tt(T.same[:, hs], T[bank][:, hs], T.hold[:, hs], A.is_equal, [bank, "hold%d" % k], ["same%d" % k])
+            elif s[0] == "c":
+                scan(T.cq[:, hs], T.keep[:, hs], T.same[:, hs], 0.0, A.mult, A.subtract, ["keep", "same%d" % k], ["cq%d" % k])
+            elif s == "C":
+                compare(on_v[done])
+                if done:
+                    total(on_v[done - 1])
+                done += 1
+            elif s == "L":
+                op("S", {"V": lambda e: e.tensor_scalar(T.pk0[:, 1:2 * J:2], T.hold[:, last], 0.0, None, A.is_lt),
+                         "S": lambda e: e.activation(T.pk0[:, 1:2 * J:2], T.hold[:, last], F.Sign, scale=-1.0)},
+                   both("hold"), ["la"])
+            elif s == "P":
+                scan(T.pk2[:], T.pk0[:], T.pk1[:], 0.0, A.mult, A.max, ["la", "lane", "tpf"], ["lc"])
+            elif s == "N":
+                copy("V", T.noff[:], T.pk2[:, 1:2 * J:2], ["lc"], ["noff"])
+            else:
+                send_h(t)
+
+        w0 = 2 * WIN * t + 8
+        wa, wb = T.wn[:, w0:w0 + L], T.wn[:, w0 + L:w0 + L + WIN]
+        ka, kb = "wa%d" % t, "wb%d" % t
+        q = HL // 2
+        place_a = [
+            lambda: join(0, NA),
+            lambda: ts(T.roff[:, 0:JH], T.cnt[:, HL - 1:HL * JH:HL], float(HL), A.add,
+                       r=["cnt%d" % j for j in range(JH)], w=["roff0"]),
+            lambda: copy("V", wa.indirect(T.roff[:, 0:JH]), T.nrow[:, 0:HL], ["nrow", "roff0"], [ka]),
+            lambda: scan(T.p2[:], wa, T.wn[:, w0 - 1:w0 + L - 1], -float(FREE * (HL + 1)), A.add, A.add, [ka], ["p2"]),
+            lambda: scan(T.ph[:], T.kbig[:], T.p2[:], 0.0, A.add, A.min, ["kbig", "p2"], ["ph"]),
+            lambda: ts(T.moff[:], T.ph[:, last], 1.0 / FREE, A.mult, HL + 0.25, A.add, r=["ph"], w=["moff"]),
+        ]
+        place_b = [
+            lambda: join(J - NB, J),
+            lambda: ts(T.roff[:, JH:J], T.cnt[:, HL * JH + q - 1:HL * JH + q * JH:q], 2.0, A.mult, float(HL + 1), A.add,
+                       r=["cnt%d" % j for j in range(JH, J)], w=["roff1"]),
+            lambda: copy("V", wb.indirect(T.roff[:, JH:J]), T.nrow[:, HL:L], ["nrow", "roff1"], [kb]),
+        ]
+        sign(on_s[0])
+        for k in range(1, len(on_s) + 1):
+            if k < len(on_s):
+                sign(on_s[k])
+            if k == NB:
+                copy("S", T.nrow[:], T.tb[:, UP - L * (t + 1):ROW[t]].indirect(T.noff[:]),
+                     ["par", "noff"] + ["new%d" % i for i in range(t + 1)] + ["row%d" % i for i in range(t)], ["nrow"])
+            sign_total(on_s[k - 1])
+            if k == 1:
+                for j0, j1 in ((0, NA), (J - NB, J)):
+                    copy("S", T.ab[:, 3 * j0 + 2:3 * j1:3], T.cq[:, 16 * j0 + 15:16 * j1:16], ["cq%d" % (j0 // JH)],
+                         ["abc%d" % (j0 // JH)])
+        for k in range(done, len(on_v) + 1):
+            if k < len(on_v):
+                compare(on_v[k])
+            if k > JH - NA:
+                place_a.pop(0)()
+            total(on_v[k - 1])
+        for b in range(4):
+            gather_top(t, b)
+        while place_a or place_b:
+            for step in place_b[:1] + place_a[:1]:
+                step()
+            place_a, place_b = place_a[1:], place_b[1:]
+        row, rk, new = T.tb[:, ROW[t + 1]:ROW[t + 1] + L], "row%d" % (t + 1), slice(C + L * t, C + L * t + L)
+        for s in END[t]:
+            k = int(s[1]) if len(s) > 1 else 0
+            if s[0] == "s":
+                tt(T["sp%d" % k][:, new], T[DB[k]][:, 0:L], T.a0[:, L * k:L * k + L], A.add, [DB[k], "a0%d" % k], ["sp%d" % k])
+            elif s[0] in "nN":
+                copy("S" if s[0] == "n" else "V", T["pp%d" % k][:, new], T[DB[k]][:, 0:L], [DB[k]], ["pp%d" % k])
+            elif s == "g":
+                tt(row, wb.indirect(T.moff[:]), wa, A.min, [ka, kb, "moff"], [rk])
+                if t == R - 1:
+                    dma("Y", T.ol[:], T.tb[0:128:16, ROW[R]:ROW[R] + L], [rk], [])
+            elif s == "h":
+                scan(T.held[:], T.kmin[:], row, 0.0, A.add, A.min, ["kmin", rk], ["held"])
+            elif s == "t":
+                ts(T["toff%d" % (t + 1)][:], T.held[:, last], T.cols[:, 0:1], A.add,
+                   r=["held", "colv"], w=both("toff%d" % (t + 1)))
+            else:
+                read_step(t + 1, s)
+
+    zp = T["zp%d" % R]
+    quant_z(R, 1)
+    copy("S", T.ya[:], T.pb0[:, 0:HL], ["pb0"], ["ya"])
+    dma("S", T.y[:, 0:HL], T.ya[:], ["ya"], [])
+    copy("V", T.yb[:], T.pb1[:, 0:HL], ["pb1"], ["yb"])
     for k in range(4):
-        dma("SY"[k // 2], T.osc[4 * k:4 * k + 4, :], zp[32 * k:32 * k + 4, :], ["zq%d0" % R, "zq%d1" % R], [])
-    dma("Y", T.y[:, hl:L], T.yb[:], ["yb"], [])
+        dma("SY"[k // 2], T.osc[4 * k:4 * k + 4, :], zp[32 * k:32 * k + 4, :], both("zq%d" % R), [])
+    dma("Y", T.y[:, HL:L], T.yb[:], ["yb"], [])
     finish("G")

from concourse.mybir import dt, AluOpType, ActivationFunctionType

A = AluOpType
F = ActivationFunctionType
C, L, R = 512, 384, 3
J = L // 16
JH, HL = J // 2, L // 2
NODES = C + R * L
NA, NB = 3, 8
FIRST = "i b y x0 k a S00 x1 x2 x3 S01 u S10 S11 S20 S21 S30 v p q0 S31".split()
FRONT = "a1 a0 a2 a3 m0 q1 r0 o0 e0 m1 r1 c0 o1 r3 r2 C e1 H c1 L C C P C N C C C".split()
END = ["n2 s1 g s0 h t s3 s2 N1 V30 n0 S10 S00 S20 S01 V31 S21 q0 N3 S11".split()] * 2 + [
    "g s0 h t S00 s1 s3 S10 s2 V30 S20 V31 S11 S21 q0 S01".split()]
ORDER = (
    "0e0a000102030405060g0h0b0j0k0u0r070n08170i0v0l0s0m0x13090q0f0p0t0c0w160d0z101114120y151c18191e0o1a1h1g1b1d1i1j1k"
    "1f1l1m1n1t1r1q1p1v1o1s1w1x1y1z201u21222324252627282d292r2a2c2e2f2b2g2h2i2j2k2l3f3b2q2s4e4b4d2t2z4h2u2x2p4i324g4n"
    "3h3e433c463d3w3q3k3t3j3o3l3v3i413n3m3x3g332v2w3140483z3r493s4442473u3y3p45394a352y3836374c4f343a4l304k4j4p4m4r4o"
    "4t4u4s4v4x4y4w4q515253545559582m575a502o5c5b4z2n5d5g5e5f5j5l5h5i5n5o5s5q5p5k5m565r5t5u6061625x635w645y655z666768"
    "695v6a6b6c6g6f8f6i6e7d6k6l6m6r6p6n6o7l878377736w8h6j8i8k766d72796t8e7x7f6u7g716v6y807o7r7h6h7a7c7b75786z8r8n8g7p"
    "7n7j8b8c887m7v7u7i7q847s867t8a8582897w7z7y818d7k8j708m6x8p747e8v8l8t8s8o8x8u8w8y8z908q919395969798999c9d9e926q9b"
    "9f6s9a949g9h9j9k9m9l9n9y9q9o9i9r9p9s9t9w9v9ua4a5a69xa1a7a0a8a2a9a3aaabacad9zaeagalafaxahamb4aibcbbakajaoapaqatbl"
    "bhc5c2btawbwbnbibrbsbpbzbyc9c3bkc0azancjb5b3bfb0bgb1avbmb8bactb9beayckcqcgb7bjcebobqc6c8cbcdccc7bvbxcabuc1cfc4bd"
    "cicocpb6chcub2crclcmcycvcxcnczcwcsd2d1d0d3d5d4d6d7d8d9dadbdcdldfddardedgdqasdiaudjdkdmdodndhdrdsdtdpdudve2dwdxdy"
    "e1dze0e3e4e5")
SWAP = (42, 63, 194, 199, 209, 210, 211, 342, 348, 357, 359, 488, 502)
DB = ("pb2", "pb3", "pb4", "pb6")
UP = R * L
ROW = [UP + C + L * t for t in range(R + 1)]
STEP = 4096.0
FREE = 2 ** 23
WIN = L + 8

SCRATCH = {
    "xs": ("sbuf", [128, 4 * C], "bfloat16"), "us": ("sbuf", [128, 512], "bfloat16"),
    "pars": ("sbuf", [128, 32], "int32"), "tops": ("sbuf", [128, J], "int32"),
    "wq": ("sbuf", [128, 512], "float8_e4m3fn_x4"), "wp": ("sbuf", [128, 512], "uint8"),
    "uq": ("sbuf", [128, 128], "float8_e4m3fn_x4"), "up": ("sbuf", [128, 128], "uint8"),
    "vq": ("sbuf", [128, 128], "float8_e4m3fn_x4"), "vp": ("sbuf", [128, 128], "uint8"),
    "et": ("sbuf", [128, 520], "bfloat16"),
    "eq": ("sbuf", [128, 512], "float8_e4m3fn_x4"), "ep": ("sbuf", [128, 512], "uint8"),
    "z": ("sbuf", [128, 4 * L], "bfloat16"), "h": ("sbuf", [128, 4 * L], "bfloat16"),
    "a0": ("sbuf", [128, 4 * L], "bfloat16"),
    "tb": ("sbuf", [128, ROW[R] + L], "float32"), "idn": ("sbuf", [128, C], "float32"),
    "wn": ("sbuf", [128, 2 * WIN * R], "float32"),
    "itp": ("sbuf", [128, 128], "int32"), "res": ("sbuf", [128, 128], "int32"), "i16": ("sbuf", [128, J], "int32"),
    "mask": ("sbuf", [128, L], "bfloat16"), "keep": ("sbuf", [128, L], "bfloat16"), "kmin": ("sbuf", [128, L], "bfloat16"),
    "kbig": ("sbuf", [128, L], "bfloat16"), "p2": ("sbuf", [128, L], "bfloat16"), "ph": ("sbuf", [128, L], "bfloat16"),
    "keep3": ("sbuf", [128, 3 * JH], "float32"), "cols": ("sbuf", [128, 8], "float32"),
    "pk0": ("sbuf", [128, 2 * J], "float32"), "pk1": ("sbuf", [128, 2 * J], "float32"),
    "pk2": ("sbuf", [128, 2 * J], "float32"),
    "uoff": ("sbuf", [128, 8], "uint16"), "po": ("sbuf", [128, 32], "uint16"),
    "noff": ("sbuf", [128, J], "uint16"), "roff": ("sbuf", [128, J], "uint16"), "moff": ("sbuf", [128, J], "uint16"),
    "mk": ("sbuf", [128, L], "float32"), "hold": ("sbuf", [128, L], "float32"),
    "same": ("sbuf", [128, L], "bfloat16"), "cq": ("sbuf", [128, L], "bfloat16"),
    "cmp": ("sbuf", [128, (L + HL) * JH], "bfloat16"), "cnt": ("sbuf", [128, (L + HL) * JH // 2], "bfloat16"),
    "ab": ("sbuf", [128, 3 * J], "float32"),
    "nrow": ("sbuf", [128, L], "float32"), "held": ("sbuf", [128, L], "float32"),
    "ya": ("sbuf", [128, HL], "float32"), "yb": ("sbuf", [128, HL], "float32"),
}
for _b in range(4):
    SCRATCH["sp%d" % _b] = ("sbuf", [128, NODES], "bfloat16")
    SCRATCH["pp%d" % _b] = ("sbuf", [128, C + 2 * L], "bfloat16")
for _t in range(R + 1):
    SCRATCH["zq%d" % _t] = ("sbuf", [128, L], "float8_e4m3fn_x4")
    SCRATCH["zp%d" % _t] = ("sbuf", [128, L], "uint8")
    SCRATCH["toff%d" % _t] = ("sbuf", [128, J], "uint16")
for _t in range(R):
    for _n in ("hq", "lq"):
        SCRATCH["%s%d" % (_n, _t)] = ("sbuf", [128, L], "float8_e4m3fn_x4")
    for _n in ("hp", "lp"):
        SCRATCH["%s%d" % (_n, _t)] = ("sbuf", [128, L], "uint8")
for _b in range(8):
    SCRATCH["pb%d" % _b] = ("psum", [128, 512], "float32")

NDMA = 16
SEMAPHORES = ["sV", "sS", "sP", "sG", "sent"] + ["arr%d" % _t for _t in range(R)] + ["d%d" % _k for _k in range(NDMA)]


def orderer(g, T):
    queue = {"V": g.vector, "S": g.scalar, "P": g.tensor, "G": g, "Y": g.sync}
    known = {q: {} for q in queue}
    count, clock, writer, readers = {}, {}, {}, {}
    noted = []

    def wait(q, marks):
        need = {}
        for sem, c in marks:
            need[sem] = max(need.get(sem, 0), c)
        for sem, c in sorted(need.items(), key=lambda e: -len(clock[e])):
            if known[q].get(sem, 0) >= c:
                continue
            queue[q].wait_ge(T.sem[sem], c)
            for s2, c2 in clock[(sem, c)].items():
                known[q][s2] = max(known[q].get(s2, 0), c2)

    def before(q, reads, writes):
        marks = []
        for k in reads:
            if k in writer:
                marks.append(writer[k])
            if k.startswith("pb"):
                marks += [m for m in readers.get(k, []) if m[0] != "s" + q]
        for k in writes:
            if k in writer and not (q == "P" and writer[k][0] == "sP"):
                marks.append(writer[k])
            marks += readers.get(k, [])
        wait(q, marks)

    def after(q, sem, n, reads, writes):
        count[sem] = count.pop(sem, 0) + n
        mark = (sem, count[sem])
        clock[mark] = dict(known[q])
        clock[mark][sem] = count[sem]
        for k in reads:
            readers.setdefault(k, []).append(mark)
        for k in writes:
            writer[k] = mark
            readers[k] = []

    def op(q, call, reads, writes):
        noted.append(["op", q, call, reads, writes])

    def dma(q, out, in_, reads, writes):
        noted.append(["dma", q, (out, in_, "d%d" % sum(e[0] == "dma" for e in noted)), reads, writes])

    def remote(call, n, reads):
        noted.append(["remote", "G", call, reads, n, None])

    def arrival(sem, n, key):
        noted[-1][5] = (sem, n, key)

    def finish(last):
        for at in range(0, len(ORDER), 2):
            i = int(ORDER[at:at + 2], 36)
            kind, q, call, reads, writes = noted[i][:5]
            if kind == "op":
                if i in SWAP:
                    q = "V" if q == "S" else "S"
                before(q, reads, writes)
                (call[q] if isinstance(call, dict) else call)(queue[q]).then_inc(T.sem["s" + q], 1)
                after(q, "s" + q, 1, reads, writes)
            elif kind == "dma":
                before(q, reads, writes)
                queue[q].dma_start(call[0], call[1]).then_inc(T.sem[call[2]], 16)
                after(q, call[2], 16, reads, writes)
            else:
                before(q, reads, [])
                call()
                after(q, "sent", writes, [], [])
                if noted[i][5]:
                    sem, n, key = noted[i][5]
                    count[sem] = n
                    clock[(sem, n)] = {sem: n}
                    writer[key] = (sem, n)
        for mark in list(count.items()):
            wait(last, [mark])

    return op, dma, remote, arrival, finish


def rank_program(g, core, T, topo):
    rank = T.rank_of(core)
    if rank is None:
        return
    n = len(T.cores)
    nxt, prv = T.cores[(rank + 1) % n], T.cores[(rank - 1) % n]
    rid, pid, _ = topo.addr(nxt)
    engines = topo.mask(core, nxt)
    n_out, n_in = len(topo.engines(core, nxt)), len(topo.engines(prv, core))
    op, dma, remote, arrival, finish = orderer(g, T)
    u8, u32 = dt.uint8, dt.uint32
    last = slice(15, L, 16)
    half = (slice(0, HL), slice(HL, L))
    lists = (slice(0, JH), slice(JH, J))
    masks = ["mask%d" % k for k in range(L // 128)]

    def both(key):
        return [key + "0", key + "1"]

    def fill(out, value, w):
        op("V", lambda e: e.memset(out, value), [], w)

    def ts(out, in0, s1, o0, s2=None, o1=None, r=(), w=()):
        if o1 is None:
            op("V", lambda e: e.tensor_scalar(out, in0, s1, None, o0), r, w)
        else:
            op("V", lambda e: e.tensor_scalar(out, in0, s1, s2, o0, o1), r, w)

    def tt(out, in0, in1, o, r, w):
        op("V", lambda e: e.tensor_tensor(out, in0, in1, o), r, w)

    def scan(out, d0, d1, init, o0, o1, r, w):
        op("V", lambda e: e.tensor_tensor_scan(out, d0, d1, init, o0, o1), r, w)

    def copy(q, out, in_, r, w):
        op(q, {"V": lambda e: e.tensor_copy(out, in_), "S": lambda e: e.activation(out, in_, F.Copy)}, r, w)

    def affine(q, out, in_, scale, bias, r, w):
        op(q, {"V": lambda e: e.tensor_scalar(out, in_, scale, bias, A.mult, A.add),
               "S": lambda e: e.activation(out, in_, F.Identity, bias=bias, scale=scale)}, r, w)

    def quant(out, scales, in_, r, w):
        op("V", lambda e: e.quantize_mx(out, scales, in_), r, w)

    def mm(bank, cols, lq, lp, rq, rp, r):
        op("P", lambda e: e.matmul_mx(T[bank][:, 0:cols], lq, lp, rq, rp, True, True), r, [bank])

    def count_up(out, cols, base, step, w):
        op("G", lambda e: e.iota(out, [[step, cols]], base, 0, allow_small_or_imprecise_dtypes=True), [], w)

    def free_places(t):
        count_up(T.wn[:, 2 * WIN * t:2 * WIN * (t + 1)], 2 * WIN, FREE, 0, ["wa%d" % t, "wb%d" % t])

    def new_numbers(t):
        count_up(T.tb[:, UP - L * (t + 1):UP - L * t], L, C + L * t, 1, ["new%d" % t])

    dma("S", T.pars[:], T.par[:], [], ["pars"])
    dma("Y", T.tops[:], T.top[:], [], ["tops"])
    dma("Y", T.xs[:], T.x[:], [], ["xs"])
    dma("Y", T.us[:], T.u[:], [], ["us"])
    dma("Y", T.wq[:].bitcast(u8), T.wc[:], [], ["wq"])
    dma("Y", T.wp[:], T.ws[:], [], ["wp"])

    op("G", lambda e: e.iota(T.itp[:], [[1, 128]], 128, -1), [], ["itp"])
    op("G", lambda e: e.iota(T.i16[:], [[16, J]], 0, 0), [], ["i16"])
    count_up(T.idn[:], C, 0, 1, ["idn"])
    free_places(0)
    fill(T.et[:], 0.0, ["et"])
    for k, v in enumerate((0.0, 1.0, 0.5)):
        fill(T.keep3[:, k:3 * JH:3], v, ["keep3%d" % k])
    fill(T.pk0[:], 0.0, ["la"])
    fill(T.ab[:, 3 * J - 2:3 * J - 1], 0.0, ["abb%d" % (J - 1)])
    ts(T.res[:], T.itp[:], 15, A.bitwise_and, r=["itp"], w=["res"])
    ts(T.et[:, 3:515:4], T.itp[:, 0:128], 128.0, A.is_equal, r=["itp", "et"], w=["et"])
    for k in range(L // 128):
        ts(T.mask[:, 128 * k:128 * k + 128], T.res[:], 0.0, A.is_equal, r=["res"], w=[masks[k]])
    ts(T.cols[:, 0:1], T.res[:, 15:16], STEP, A.mult, r=["res"], w=["colv"])
    ts(T.cols[:, 1:2], T.res[:, 15:16], -1.0, A.mult, 15.0, A.add, r=["res"], w=["colp"])
    copy("V", T.uoff[:], T.i16[:, 0:8], ["i16"], ["uoff"])
    affine("S", T.keep[:], T.mask[:], -1.0, 1.0, masks, ["keep"])
    ts(T.cols[:, 4:4 + R], T.i16[:, 1:1 + R], L / 16.0, A.mult, T.cols[:, 0:1], A.add, r=["i16", "colv"], w=["colt"])
    ts(T.pk1[:, 1:2 * J:2], T.i16[:], T.cols[:, 1:2], A.add, r=["i16", "colp"], w=["lane"])
    copy("V", T.po[:], T.pars[:], ["pars"], ["po"])
    copy("V", T.toff0[:], T.tops[:], ["tops"], both("toff0"))
    ts(T.pk1[:, 0:2 * J:2], T.tops[:], float(L), A.add, r=["tops"], w=["tpf"])
    for b in range(4):
        quant(T.eq[:, 128 * b:128 * b + 128], T.ep[:, 128 * b:128 * b + 128], T.et[:, 3 - b:515 - b], ["et"], ["eq%d" % b])

    def gather_z(q, t, b, k):
        copy(q, T.z[:, 4 * HL * k + b:4 * HL * (k + 1):4], T["sp%d" % b][:, 0:C + L * t].indirect(T["toff%d" % t][:, lists[k]]),
             ["sp%d" % b, "toff%d%d" % (t, k)], ["z%d%d" % (b, k)])

    def gather_top(t, b):
        copy("S", T.a0[:, L * b:L * b + L], T["pp%d" % b][:, 0:C + L * t].indirect(T["toff%d" % t][:]),
             ["pp%d" % b] + both("toff%d" % t), ["a0%d" % b])

    def layer(t, k):
        for b in range(4):
            mm("pb%d" % (2 + b), HL, T.wq[:, 128 * b:128 * b + 128], T.wp[:, 128 * b:128 * b + 128],
               T["zq%d" % t][:, half[k]], T["zp%d" % t][:, half[k]], ["wq", "wp", "zq%d%d" % (t, k)])

    def relu(b, k):
        out, in_ = T.h[:, 4 * HL * k + b:4 * HL * (k + 1):4], T["pb%d" % (2 + b)][:, 0:HL]
        op("S", {"V": lambda e: e.tensor_scalar(out, in_, 0.0, 0.015625, A.max, A.mult),
                 "S": lambda e: e.activation(out, in_, F.Relu, scale=0.015625)}, ["pb%d" % (2 + b)], ["h%d%d" % (b, k)])

    def quant_z(t, k):
        zq, zp = T["zq%d" % t], T["zp%d" % t]
        quant(zq[:, half[k]], zp[:, half[k]], T.z[:, 4 * HL * k:4 * HL * (k + 1)], ["z%d%d" % (b, k) for b in range(4)],
              ["zq%d%d" % (t, k)])
        if t == R:
            mm("pb%d" % k, HL, T.uq[:], T.up[:], zq[:, half[k]], zp[:, half[k]], ["uq", "zq%d%d" % (t, k)])
            dma("Y", T.oc[:, 4 * HL * k:4 * HL * (k + 1)], zq[:, half[k]].bitcast(u8), ["zq%d%d" % (t, k)], [])
        elif k == 0:
            mm("pb7", HL, T.vq[:], T.vp[:], zq[:, half[0]], zp[:, half[0]], ["vq", "vp", "zq%d0" % t])
            layer(t, 0)
        else:
            zn = both("zq%d" % t)
            mm("pb0", L, T.vq[:], T.vp[:], zq[:], zp[:], ["vq", "vp"] + zn)
            layer(t, 1)
            mm("pb1", L, T.vq[:], T.vp[:], zq[:], zp[:], ["vq", "vp"] + zn)

    def read_step(t, s):
        if s[0] in "SV":
            gather_z(s[0], t, int(s[1]), int(s[2]))
        else:
            quant_z(t, int(s[1]))

    copy("V", T.pp0[:, 0:C], T.xs[:, 0:4 * C:4], ["xs"], ["pp0"])
    for b in (2, 3):
        op("G", lambda e, b=b: e.affine_select(T["pp%d" % b][:, 0:C], T.xs[:, b:4 * C:4], [[1, C]], A.is_ge, 0.0, 0, 0),
           ["xs"], ["pp%d" % b])
    new_numbers(0)
    for s in FIRST:
        if s[0] == "x":
            b = int(s[1])
            tt(T["sp%d" % b][:, 0:C], T["pp%d" % b][:, 0:C].indirect(T.po[:]), T.xs[:, b:4 * C:4], A.add,
               ["xs", "po", "pp%d" % b], ["sp%d" % b])
        elif s == "y":
            copy("S", T.pp1[:, 0:C], T.xs[:, 1:4 * C:4], ["xs"], ["pp1"])
        elif s == "i":
            affine("S", T.kmin[:], T.mask[:], 18 * STEP, -STEP, masks, ["kmin"])
        elif s == "k":
            affine("S", T.kbig[:], T.mask[:], 1024.0 * FREE, 0.0, masks, ["kbig"])
        elif s == "a":
            copy("S", T.tb[:, UP:UP + C], T.idn[:].indirect(T.po[:]), ["idn", "po"], ["par"])
        elif s == "b":
            copy("S", T.tb[:, ROW[0]:ROW[0] + L], T.idn[:].indirect(T.toff0[:]), ["idn"] + both("toff0"), ["row0"])
        elif s == "u":
            quant(T.uq[:], T.up[:], T.us[:], ["us"], ["uq"])
        elif s == "p":
            copy("S", T.vp[:], T.up[:].indirect(T.uoff[:]), ["uq", "uoff"], ["vp"])
        elif s == "v":
            copy("V", T.vq[:].bitcast(u32), T.uq[:].bitcast(u32).indirect(T.uoff[:]), ["uq", "uoff"], ["vq"])
        else:
            read_step(0, s)

    s0, s1 = T.pb0, T.pb1
    on_s = list(range(NA)) + list(range(J - NB, J))
    on_v = [j for j in range(J) if j not in on_s]

    def span(j):
        lo = 0 if j < JH else HL
        return lo, 16 * j + 16, (L * j if j < JH else L * JH + HL * (j - JH)) - lo

    def compare(j):
        lo, mid, base = span(j)
        own, hk = T.hold[:, mid - 1:mid], "hold%d" % (j // JH)
        ts(T.cmp[:, base + lo:base + mid], s0[:, lo:mid], own, A.is_ge, -0.5, A.add, r=["pb0", hk], w=["ca%d" % j])
        ts(T.cmp[:, base + mid:base + L], s0[:, mid:L], own, A.is_gt, -0.5, A.add, r=["pb0", hk], w=["cb%d" % j])

    def total(j):
        lo, mid, base = span(j)
        w, at = (L - lo) // 2, (base + lo) // 2
        scan(T.cnt[:, at:at + w], T.cmp[:, 2 * at:2 * at + w], T.cmp[:, 2 * at + w:2 * at + 2 * w],
             T.cq[:, mid - 1:mid], A.add, A.add, ["ca%d" % j, "cb%d" % j, "cq%d" % (j // JH)], ["cnt%d" % j])

    def sign(j):
        lo, mid, base = span(j)
        op("S", lambda e: e.activation(T.cmp[:, base + lo:base + L], s1[:, lo:L], F.Sign,
                                       bias=T.hold[:, mid - 1:mid], scale=-1.0),
           ["pb1", "hold%d" % (j // JH)], ["ca%d" % j, "cb%d" % j])

    def sign_total(j):
        lo, mid, base = span(j)
        v, v2 = T.cmp[:, base + lo:base + mid], T.cmp[:, base + mid:base + L]
        op("S", lambda e: e.activation(v, v, F.Sign, bias=0.5, scale=-1.0, accum_out=T.ab[:, 3 * j:3 * j + 1]),
           ["ca%d" % j], ["ca%d" % j, "aba%d" % j])
        if mid < L:
            op("S", lambda e: e.activation(v2, v2, F.Sign, bias=-0.5, scale=-1.0, accum_out=T.ab[:, 3 * j + 1:3 * j + 2]),
               ["cb%d" % j], ["cb%d" % j, "abb%d" % j])

    def join(j0, j1):
        lo, _, base = span(j0)
        at, third = (base + lo) // 2, (L - lo) // 6
        scan(T.cnt[:, at + third - 1:at + 3 * third * (j1 - j0):third], T.keep3[:, 0:3 * (j1 - j0)], T.ab[:, 3 * j0:3 * j1],
             0.0, A.mult, A.add,
             ["keep30", "keep31", "keep32", "abc%d" % (j0 // JH)] + ["ab%s%d" % (c, j) for c in "ab" for j in range(j0, j1)],
             ["cnt%d" % j for j in range(j0, j1)])

    def send_h(t):
        hq, hp, lq, lp, arr = T["hq%d" % t], T["hp%d" % t], T["lq%d" % t], T["lp%d" % t], T.sem["arr%d" % t]
        quant(hq[:], hp[:], T.h[:], ["h%d%d" % (b, k) for b in range(4) for k in range(2)], ["hq%d" % t])
        remote(lambda: g.remote_dma(lq[:].bitcast(u8), hq[:].bitcast(u8), arr, T.sem.sent, pid, rid, engines), n_out, ["hq%d" % t])
        remote(lambda: g.remote_dma(lp[:], hp[:], arr, T.sem.sent, pid, rid, engines), n_out, ["hq%d" % t])
        arrival("arr%d" % t, 2 * n_in, "land%d" % t)
        if t < R - 1:
            free_places(t + 1)
            new_numbers(t + 1)
        for b in range(4):
            mm(DB[b], L, T.eq[:, 128 * b:128 * b + 128], T.ep[:, 128 * b:128 * b + 128], lq[:], lp[:],
               ["eq%d" % b, "land%d" % t])

    for t in range(R):
        if t > 0:
            affine("S", T.pk1[:, 0:2 * J:2], T.held[:, last], 1.0, T.cols[:, 4 + t:5 + t], ["held", "colt"], ["tpf"])
        done = 0
        for s in FRONT:
            k = int(s[1]) if len(s) > 1 else 0
            bank, hs = ("pb7", "pb0")[k % 2], half[k % 2]
            if s[0] == "q":
                quant_z(t, k)
            elif s[0] in "ar":
                relu(k, "ar".index(s[0]))
            elif s[0] == "m":
                tt(T.mk[:, hs], T[bank][:, hs], T.mask[:, hs], A.mult, [bank] + masks, ["mk%d" % k])
            elif s[0] == "o":
                scan(T.hold[:, hs], T.keep[:, hs], T.mk[:, hs], 0.0, A.mult, A.add, ["keep", "mk%d" % k], ["hold%d" % k])
            elif s[0] == "e":
                tt(T.same[:, hs], T[bank][:, hs], T.hold[:, hs], A.is_equal, [bank, "hold%d" % k], ["same%d" % k])
            elif s[0] == "c":
                scan(T.cq[:, hs], T.keep[:, hs], T.same[:, hs], 0.0, A.mult, A.subtract, ["keep", "same%d" % k], ["cq%d" % k])
            elif s == "C":
                compare(on_v[done])
                if done:
                    total(on_v[done - 1])
                done += 1
            elif s == "L":
                op("S", {"V": lambda e: e.tensor_scalar(T.pk0[:, 1:2 * J:2], T.hold[:, last], 0.0, None, A.is_lt),
                         "S": lambda e: e.activation(T.pk0[:, 1:2 * J:2], T.hold[:, last], F.Sign, scale=-1.0)},
                   both("hold"), ["la"])
            elif s == "P":
                scan(T.pk2[:], T.pk0[:], T.pk1[:], 0.0, A.mult, A.max, ["la", "lane", "tpf"], ["lc"])
            elif s == "N":
                copy("V", T.noff[:], T.pk2[:, 1:2 * J:2], ["lc"], ["noff"])
            else:
                send_h(t)

        w0 = 2 * WIN * t + 8
        wa, wb = T.wn[:, w0:w0 + L], T.wn[:, w0 + L:w0 + L + WIN]
        ka, kb = "wa%d" % t, "wb%d" % t
        q = HL // 2
        place_a = [
            lambda: join(0, NA),
            lambda: ts(T.roff[:, 0:JH], T.cnt[:, HL - 1:HL * JH:HL], float(HL), A.add,
                       r=["cnt%d" % j for j in range(JH)], w=["roff0"]),
            lambda: copy("V", wa.indirect(T.roff[:, 0:JH]), T.nrow[:, 0:HL], ["nrow", "roff0"], [ka]),
            lambda: scan(T.p2[:], wa, T.wn[:, w0 - 1:w0 + L - 1], -float(FREE * (HL + 1)), A.add, A.add, [ka], ["p2"]),
            lambda: scan(T.ph[:], T.kbig[:], T.p2[:], 0.0, A.add, A.min, ["kbig", "p2"], ["ph"]),
            lambda: ts(T.moff[:], T.ph[:, last], 1.0 / FREE, A.mult, HL + 0.25, A.add, r=["ph"], w=["moff"]),
        ]
        place_b = [
            lambda: join(J - NB, J),
            lambda: ts(T.roff[:, JH:J], T.cnt[:, HL * JH + q - 1:HL * JH + q * JH:q], 2.0, A.mult, float(HL + 1), A.add,
                       r=["cnt%d" % j for j in range(JH, J)], w=["roff1"]),
            lambda: copy("V", wb.indirect(T.roff[:, JH:J]), T.nrow[:, HL:L], ["nrow", "roff1"], [kb]),
        ]
        sign(on_s[0])
        for k in range(1, len(on_s) + 1):
            if k < len(on_s):
                sign(on_s[k])
            if k == NB:
                copy("S", T.nrow[:], T.tb[:, UP - L * (t + 1):ROW[t]].indirect(T.noff[:]),
                     ["par", "noff"] + ["new%d" % i for i in range(t + 1)] + ["row%d" % i for i in range(t)], ["nrow"])
            sign_total(on_s[k - 1])
            if k == 1:
                for j0, j1 in ((0, NA), (J - NB, J)):
                    copy("S", T.ab[:, 3 * j0 + 2:3 * j1:3], T.cq[:, 16 * j0 + 15:16 * j1:16], ["cq%d" % (j0 // JH)],
                         ["abc%d" % (j0 // JH)])
        for k in range(done, len(on_v) + 1):
            if k < len(on_v):
                compare(on_v[k])
            if k > JH - NA:
                place_a.pop(0)()
            total(on_v[k - 1])
        for b in range(4):
            gather_top(t, b)
        while place_a or place_b:
            for step in place_b[:1] + place_a[:1]:
                step()
            place_a, place_b = place_a[1:], place_b[1:]
        row, rk, new = T.tb[:, ROW[t + 1]:ROW[t + 1] + L], "row%d" % (t + 1), slice(C + L * t, C + L * t + L)
        for s in END[t]:
            k = int(s[1]) if len(s) > 1 else 0
            if s[0] == "s":
                tt(T["sp%d" % k][:, new], T[DB[k]][:, 0:L], T.a0[:, L * k:L * k + L], A.add, [DB[k], "a0%d" % k], ["sp%d" % k])
            elif s[0] in "nN":
                copy("S" if s[0] == "n" else "V", T["pp%d" % k][:, new], T[DB[k]][:, 0:L], [DB[k]], ["pp%d" % k])
            elif s == "g":
                tt(row, wb.indirect(T.moff[:]), wa, A.min, [ka, kb, "moff"], [rk])
                if t == R - 1:
                    dma("Y", T.ol[:], T.tb[0:128:16, ROW[R]:ROW[R] + L], [rk], [])
            elif s == "h":
                scan(T.held[:], T.kmin[:], row, 0.0, A.add, A.min, ["kmin", rk], ["held"])
            elif s == "t":
                ts(T["toff%d" % (t + 1)][:], T.held[:, last], T.cols[:, 0:1], A.add,
                   r=["held", "colv"], w=both("toff%d" % (t + 1)))
            else:
                read_step(t + 1, s)

    zp = T["zp%d" % R]
    quant_z(R, 1)
    copy("S", T.ya[:], T.pb0[:, 0:HL], ["pb0"], ["ya"])
    dma("S", T.y[:, 0:HL], T.ya[:], ["ya"], [])
    copy("V", T.yb[:], T.pb1[:, 0:HL], ["pb1"], ["yb"])
    for k in range(4):
        dma("SY"[k // 2], T.osc[4 * k:4 * k + 4, :], zp[32 * k:32 * k + 4, :], both("zq%d" % R), [])
    dma("Y", T.y[:, HL:L], T.yb[:], ["yb"], [])
    finish("G")
